import numpy as np
import ml_dtypes


def mxq(x, axis, fmt="e4m3"):
    dtype, down = {"e4m3": (ml_dtypes.float8_e4m3fn, 7), "e5m2": (ml_dtypes.float8_e5m2, 14)}[fmt]
    v = np.moveaxis(np.asarray(x, np.float32).astype(ml_dtypes.bfloat16).astype(np.float64), axis, -1)
    blocks = v.reshape(v.shape[:-1] + (-1, 32))
    amax = np.abs(blocks).max(-1, keepdims=True)
    byte = np.maximum(np.where(amax > 0, np.frexp(amax)[1] - 1 + 127, 0) - down, 1)
    scale = np.exp2(byte - 127.0)
    codes = (blocks / scale).astype(np.float32).astype(dtype).astype(np.float64)
    return np.moveaxis((codes * scale).reshape(v.shape), -1, axis)


WIDE = False


def mx_kscale(k):
    if not WIDE:
        return np.ones(k)
    levels = np.array([10, -10, 5, -5, 0])
    if k % 512:
        return np.exp2(np.random.permutation(np.resize(levels, k // 32))).repeat(32)
    a = np.empty((k // 512, 16))
    for p in range(k // 512):
        a[p, :8] = np.random.permutation(np.resize(levels, 8))
        for g in range(8):
            far = levels[np.abs(levels - a[p, g]) >= 10]
            a[p, g + 8] = far[np.random.randint(len(far))]
    return np.exp2(a.ravel()).repeat(32)


def f64(x):
    return np.asarray(x).astype(np.float64)


def striped(idx):
    return np.tile(idx.reshape(-1, 16).T, (8, 1)).astype(np.uint16)


def unstriped(offs):
    return offs[:16].T.reshape(-1).astype(np.int64)


def pack_weight(w):
    k, n = w.shape
    w = f64(np.asarray(w, np.float32).astype(ml_dtypes.bfloat16)).reshape(k // 32, 32, n)
    amax = np.abs(w).max(1)
    byte = np.clip(np.where(amax > 0, np.frexp(amax)[1] - 1 + 127 - 7, 1), 1, 254)
    scaled = (w * np.exp2(127.0 - byte)[:, None, :]).reshape(k, n).astype(np.float32)
    words = np.ascontiguousarray(scaled.reshape(k // 512, 128, 4, n).transpose(0, 1, 3, 2)).astype(ml_dtypes.float8_e4m3fn).view(np.uint8)
    return words, np.ascontiguousarray(byte.astype(np.uint8).reshape(k // 512, 16, n))


def unpack_weight(words, scales):
    g, p, n, _ = words.shape
    vals = np.ascontiguousarray(words).view(ml_dtypes.float8_e4m3fn).astype(np.float64) * np.repeat(np.exp2(scales.astype(np.float64) - 127.0), 8, axis=1)[..., None]
    return vals.transpose(0, 1, 3, 2).reshape(g * 512, n)


def relu(v):
    return np.maximum(v, 0.0)


K, T, S, V, N = 512, 4096, 1024, 512, 256


def setup_inputs():
    n = np.random.standard_normal
    s = mx_kscale(K)[:, None]
    packed_xT = pack_weight(n((K, T)) * s)
    return {
        "x_words": packed_xT[0],
        "x_scales": packed_xT[1],
        "w1": (n((K, N)) / np.sqrt(K) / s).astype(np.float32),
        "w2": (n((K, N)) / np.sqrt(K) / s).astype(np.float32),
        "w3": (n((K, N)) / np.sqrt(K) / s).astype(np.float32),
        "offs": striped(np.random.permutation(T)[:S]),
        "cen": striped(np.random.permutation(S)[:V]),
        "pos1": striped(np.random.permutation(S)[:V]),
        "pos2": striped(np.random.permutation(S)[:V]),
        "pos3": striped(np.random.permutation(S)[:V]),
    }


def reference(x_words, x_scales, w1, w2, w3, offs, cen, pos1, pos2, pos3):
    xq = unpack_weight(x_words, x_scales)[:, unstriped(offs)]
    h = mxq(f64(w3), 0, "e4m3").T @ xq
    g = mxq(f64(w1), 0, "e4m3").T @ xq
    gc = g[:, unstriped(cen)]
    s = mxq(f64(w2), 0, "e4m3").T @ xq
    sc = s[:, unstriped(cen)]
    return relu(h[:, unstriped(pos1)] * gc + sc) + relu(h[:, unstriped(pos2)] * gc + sc) + relu(h[:, unstriped(pos3)] * gc + sc)

@@ -1,0 +1,221 @@
+from contextlib import ExitStack
+
+import concourse.mybir as mybir
+from concourse.masks import make_identity
+
+K, T, S, V, N = 512, 4096, 1024, 512, 256
+FLOPS = 3 * 2 * K * N * S
+
+F32 = mybir.dt.float32
+BF16 = mybir.dt.bfloat16
+I32 = mybir.dt.int32
+U32 = mybir.dt.uint32
+U16 = mybir.dt.uint16
+U8 = mybir.dt.uint8
+FP8X4 = mybir.dt.float8_e4m3fn_x4
+RELU = mybir.ActivationFunctionType.Relu
+MULT = mybir.AluOpType.mult
+ADD = mybir.AluOpType.add
+MAX = mybir.AluOpType.max
+
+P = 128
+PACK = 4
+BANK = 512
+SCALE_ROWS = 16
+LIST_GROUP = 16
+
+
+def tile_picked_filmg_relu_p_kernel(
+    tc, x_words, x_scales, w1, w2, w3, offs, cen, pos1, pos2, pos3, out
+):
+    nc = tc.nc
+    with ExitStack() as ctx:
+        sb = ctx.enter_context(tc.tile_pool(name="sb", bufs=1))
+        ps = ctx.enter_context(tc.psum_pool(name="ps", bufs=1))
+
+        def bank_tile(b):
+            return ps.tile([P, BANK], F32, name="bank%d" % b)
+
+        first = P - SCALE_ROWS
+        scale_table = sb.tile([P, T], U8, name="scale_table", align_bytes=64)
+        nc.sync.dma_start(out=scale_table[first:P, :].bitcast(I32), in_=x_scales[0].bitcast(I32))
+        lists = {}
+        for name, src in (("offs", offs), ("cen", cen), ("pos1", pos1), ("pos2", pos2), ("pos3", pos3)):
+            lists[name] = sb.tile(list(src.shape), U16, name="list_" + name)
+            nc.sync.dma_start(lists[name][:], src)
+        word_table = sb.tile([P, T], I32, name="word_table", align_bytes=64)
+        nc.sync.dma_start(out=word_table[:], in_=x_words[0].rearrange("p n t -> p (n t)").bitcast(I32))
+        raw = {}
+        for name, src in (("g", w1), ("s", w2), ("h", w3)):
+            raw[name] = sb.tile([P, PACK, N], F32, name="raw_" + name)
+            nc.sync.dma_start(out=raw[name][:], in_=src.rearrange("(p j) n -> p j n", j=PACK))
+
+        nc.vector.memset(scale_table[0:first, :].bitcast(I32), 0)
+        ident_raw = sb.tile([P, P], F32, name="ident_raw", tag="x_plane", align_bytes=64)
+        make_identity(nc, ident_raw[:])
+        ident = sb.tile([P, P], F32, name="ident")
+        nc.scalar.activation(ident[:], ident_raw[:], RELU)
+        x_plane = sb.tile([P, S], U8, name="x_plane", tag="x_plane", align_bytes=64)
+        nc.vector.memset(x_plane[:].bitcast(I32), 0)
+
+        picked_scales = sb.tile([P, S], U8, name="picked_scales", align_bytes=64)
+        nc.vector.tensor_copy(picked_scales[:], scale_table[:].indirect(lists["offs"][:]))
+        for q in range(4):
+            nc.scalar.dma_start(
+                out=x_plane[32 * q : 32 * q + 4, :].bitcast(I32),
+                in_=picked_scales[first + 4 * q : first + 4 * q + 4, :].bitcast(I32),
+            )
+
+        x_codes = []
+
+        def pick_words(half):
+            codes = sb.tile([P, BANK], U32, name="x_codes%d" % half, align_bytes=64)
+            cols = BANK // LIST_GROUP
+            nc.vector.tensor_copy(
+                codes[:], word_table[:].bitcast(U32).indirect(lists["offs"][:, half * cols : (half + 1) * cols])
+            )
+            x_codes.append(codes)
+
+        grouped, w_codes, w_plane, rows = {}, {}, {}, {}
+
+        def cast(name, blk, engine_copy):
+            grouped[name, blk] = sb.tile([P, P, PACK], BF16, name="grp_%s%d" % (name, blk), align_bytes=64)
+            engine_copy(
+                grouped[name, blk][:].rearrange("p (c i) t -> p c t i", i=4),
+                raw[name][:, :, blk * P : (blk + 1) * P].rearrange("p t (c i) -> p c t i", i=4),
+            )
+
+        def quantize(name, blk):
+            w_codes[name, blk] = sb.tile([P, P], U32, name="wc_%s%d" % (name, blk), align_bytes=64)
+            w_plane[name, blk] = sb.tile([P, P], U8, name="wp_%s%d" % (name, blk), align_bytes=64)
+            nc.vector.quantize_mx(
+                out=w_codes[name, blk][:].bitcast(FP8X4),
+                scales=w_plane[name, blk][:],
+                in_=grouped[name, blk][:].rearrange("p c t -> p (c t)"),
+            )
+
+        def product(name, blk, half, b, engine_copy):
+            if (name, blk) not in rows:
+                rows[name, blk] = sb.tile([P, S], F32, name="rows_%s%d" % (name, blk))
+            cols = slice(half * BANK, (half + 1) * BANK)
+            bank = bank_tile(b)
+            nc.tensor.matmul_mx(
+                out=bank[:],
+                lhsT=w_codes[name, blk][:].bitcast(FP8X4),
+                lhsT_scale=w_plane[name, blk][:],
+                rhs=x_codes[half][:].bitcast(FP8X4),
+                rhs_scale=x_plane[:, cols],
+                start=True,
+                stop=True,
+            )
+            engine_copy(rows[name, blk][:, cols], bank[:])
+
+        at_cen = {}
+
+        def centre(name, blk):
+            at_cen[name, blk] = sb.tile([P, V], F32, name="cen_%s%d" % (name, blk))
+            nc.vector.tensor_copy(at_cen[name, blk][:], rows[name, blk][:].indirect(lists["cen"][:]))
+
+        def scaled(blk, d, c0, c1):
+            u = sb.tile([P, c1 - c0], F32, name="u_%d_%d_%d" % (blk, d, c0))
+            offsets = lists["pos%d" % (d + 1)][:, c0 // LIST_GROUP : c1 // LIST_GROUP]
+            nc.vector.tensor_tensor(u[:], rows["h", blk][:].indirect(offsets), at_cen["g", blk][:, c0:c1], MULT)
+            return u
+
+        def turn(bank, src, n, start, stop):
+            for j in range(n // P):
+                nc.tensor.matmul(
+                    bank[:, j * P : (j + 1) * P],
+                    lhsT=src[:, j * P : (j + 1) * P],
+                    rhs=ident[:],
+                    is_transpose=True,
+                    start=start and j == 0,
+                    stop=stop and j == n // P - 1,
+                )
+
+        def relu_of(z, name):
+            r = sb.tile([P, BANK], F32, name=name)
+            nc.scalar.activation(r[:], z[:], RELU)
+            return r
+
+        vcopy, scopy = nc.vector.tensor_copy, nc.scalar.copy
+        H = V // 2
+
+        pick_words(0)
+        cast("g", 0, scopy)
+        pick_words(1)
+        quantize("g", 0)
+        cast("g", 1, scopy)
+        cast("s", 0, scopy)
+        product("g", 0, 0, 0, scopy)
+        quantize("g", 1)
+        cast("s", 1, vcopy)
+        quantize("s", 0)
+        cast("h", 0, vcopy)
+        product("g", 0, 1, 1, vcopy)
+        quantize("s", 1)
+        quantize("h", 0)
+        product("s", 0, 0, 2, scopy)
+        product("s", 0, 1, 3, scopy)
+        centre("g", 0)
+        product("h", 0, 0, 4, scopy)
+        product("h", 0, 1, 5, scopy)
+        centre("s", 0)
+        cast("h", 1, scopy)
+        product("g", 1, 0, 6, scopy)
+        product("g", 1, 1, 7, scopy)
+        quantize("h", 1)
+        product("s", 1, 0, 0, scopy)
+        product("s", 1, 1, 1, scopy)
+
+        acc0 = bank_tile(7)
+        for d in range(3):
+            if d == 2:
+                product("h", 1, 0, 2, scopy)
+                product("h", 1, 1, 3, scopy)
+            u = scaled(0, d, 0, V)
+            z = bank_tile(4 + d)
+            turn(z, at_cen["s", 0], V, True, False)
+            turn(z, u, V, False, True)
+            r = relu_of(z, "r0%d" % d)
+            turn(acc0, r, V, d == 0, d == 2)
+        res0 = sb.tile([P, V], F32, name="res0")
+        nc.scalar.copy(res0[:], acc0[:])
+        nc.scalar.dma_start(out=out[0:P, :], in_=res0[:])
+
+        centre("g", 1)
+        centre("s", 1)
+        shift = at_cen["s", 1]
+        u = scaled(1, 0, 0, V)
+        z = bank_tile(6)
+        turn(z, shift, V, True, False)
+        turn(z, u, V, False, True)
+        r10 = relu_of(z, "r10")
+        z = bank_tile(7)
+        turn(z[:, 0:H], shift, H, True, False)
+        turn(z[:, H:V], shift, H, False, False)
+        for d in (1, 2):
+            u = scaled(1, d, 0, H)
+            turn(z[:, (d - 1) * H : d * H], u, H, False, d == 2)
+        acc_b = bank_tile(0)
+        turn(acc_b, r10[:, H:V], H, True, True)
+        acc_a = bank_tile(1)
+        turn(acc_a, r10[:, 0:H], H, True, False)
+        r = relu_of(z, "r1a")
+        turn(acc_a, r[:, 0:H], H, False, False)
+        turn(acc_a, r[:, H:V], H, False, True)
+        res_a = sb.tile([P, H], F32, name="res_a")
+        nc.scalar.copy(res_a[:], acc_a[:, 0:H])
+        nc.scalar.dma_start(out=out[P : 2 * P, 0:H], in_=res_a[:])
+
+        us = [scaled(1, d, H, V) for d in (1, 2)]
+        zs = []
+        for d, u in enumerate(us):
+            z = sb.tile([P, H], F32, name="z_tail%d" % d)
+            nc.vector.tensor_tensor(z[:], u[:], shift[:, H:V], ADD)
+            zs.append(z)
+        part = sb.tile([P, H], F32, name="part")
+        nc.vector.scalar_tensor_tensor(part[:], zs[0][:], 0.0, acc_b[:, 0:H], MAX, ADD)
+        res_b = sb.tile([P, H], F32, name="res_b")
+        nc.vector.scalar_tensor_tensor(res_b[:], zs[1][:], 0.0, part[:], MAX, ADD)
+        nc.sync.dma_start(out=out[P : 2 * P, H:V], in_=res_b[:])

@@ -31,40 +31,53 @@ def tile_picked_filmg_relu_p_kernel(
     nc = tc.nc
     with ExitStack() as ctx:
         sb = ctx.enter_context(tc.tile_pool(name="sb", bufs=1))
+        lap = ctx.enter_context(tc.tile_pool(name="lap", bufs=1))
         ps = ctx.enter_context(tc.psum_pool(name="ps", bufs=1))
 
         def bank_tile(b):
             return ps.tile([P, BANK], F32, name="bank%d" % b)
 
         first = P - SCALE_ROWS
-        scale_table = sb.tile([P, T], U8, name="scale_table", align_bytes=64)
+        scale_table = lap.tile([P, T], U8, name="scale_table", offset=T // 2 + 32)
         nc.sync.dma_start(out=scale_table[first:P, :].bitcast(I32), in_=x_scales[0].bitcast(I32))
         lists = {}
-        for name, src in (("offs", offs), ("cen", cen), ("pos1", pos1), ("pos2", pos2), ("pos3", pos3)):
+
+        def load_list(name, src):
             lists[name] = sb.tile(list(src.shape), U16, name="list_" + name)
             nc.sync.dma_start(lists[name][:], src)
+
+        raw = {}
+
+        def load_weights(name, src, dst):
+            nc.sync.dma_start(out=dst[:], in_=src.rearrange("(p j) n -> p j n", j=PACK))
+            for blk in range(2):
+                raw[name, blk] = dst[:, :, blk * P : (blk + 1) * P]
+
+        load_list("offs", offs)
+        load_weights("g", w1, sb.tile([P, PACK, N], F32, name="raw_g"))
+        for name, src in (("cen", cen), ("pos1", pos1), ("pos2", pos2)):
+            load_list(name, src)
         word_table = sb.tile([P, T], I32, name="word_table", align_bytes=64)
         nc.sync.dma_start(out=word_table[:], in_=x_words[0].rearrange("p n t -> p (n t)").bitcast(I32))
-        raw = {}
-        for name, src in (("g", w1), ("s", w2), ("h", w3)):
-            raw[name] = sb.tile([P, PACK, N], F32, name="raw_" + name)
-            nc.sync.dma_start(out=raw[name][:], in_=src.rearrange("(p j) n -> p j n", j=PACK))
+        load_list("pos3", pos3)
 
         nc.vector.memset(scale_table[0:first, :].bitcast(I32), 0)
-        ident_raw = sb.tile([P, P], F32, name="ident_raw", tag="x_plane", align_bytes=64)
+        ident_raw = sb.tile([P, P], F32, name="ident_raw")
         make_identity(nc, ident_raw[:])
         ident = sb.tile([P, P], F32, name="ident")
         nc.scalar.activation(ident[:], ident_raw[:], RELU)
-        x_plane = sb.tile([P, S], U8, name="x_plane", tag="x_plane", align_bytes=64)
+        x_plane = sb.tile([P, S], U8, name="x_plane", align_bytes=64)
         nc.vector.memset(x_plane[:].bitcast(I32), 0)
 
         picked_scales = sb.tile([P, S], U8, name="picked_scales", align_bytes=64)
         nc.vector.tensor_copy(picked_scales[:], scale_table[:].indirect(lists["offs"][:]))
         for q in range(4):
-            nc.scalar.dma_start(
+            nc.sync.dma_start(
                 out=x_plane[32 * q : 32 * q + 4, :].bitcast(I32),
                 in_=picked_scales[first + 4 * q : first + 4 * q + 4, :].bitcast(I32),
             )
+        load_weights("s", w2, lap.tile([P, PACK, N], F32, name="raw_s", offset=32))
+        load_weights("h", w3, lap.tile([P, PACK, N], F32, name="raw_h", offset=T + 32))
 
         x_codes = []
 
@@ -82,7 +95,7 @@ def tile_picked_filmg_relu_p_kernel(
             grouped[name, blk] = sb.tile([P, P, PACK], BF16, name="grp_%s%d" % (name, blk), align_bytes=64)
             engine_copy(
                 grouped[name, blk][:].rearrange("p (c i) t -> p c t i", i=4),
-                raw[name][:, :, blk * P : (blk + 1) * P].rearrange("p t (c i) -> p c t i", i=4),
+                raw[name, blk].rearrange("p t (c i) -> p c t i", i=4),
             )
 
         def quantize(name, blk):
@@ -94,26 +107,35 @@ def tile_picked_filmg_relu_p_kernel(
                 in_=grouped[name, blk][:].rearrange("p c t -> p (c t)"),
             )
 
-        def product(name, blk, half, b, engine_copy):
-            if (name, blk) not in rows:
-                rows[name, blk] = sb.tile([P, S], F32, name="rows_%s%d" % (name, blk))
-            cols = slice(half * BANK, (half + 1) * BANK)
-            bank = bank_tile(b)
+        banks = {}
+
+        def product(name, blk, half, b):
+            banks[name, blk, half] = bank_tile(b)
             nc.tensor.matmul_mx(
-                out=bank[:],
+                out=banks[name, blk, half][:],
                 lhsT=w_codes[name, blk][:].bitcast(FP8X4),
                 lhsT_scale=w_plane[name, blk][:],
                 rhs=x_codes[half][:].bitcast(FP8X4),
-                rhs_scale=x_plane[:, cols],
+                rhs_scale=x_plane[:, half * BANK : (half + 1) * BANK],
                 start=True,
                 stop=True,
             )
-            engine_copy(rows[name, blk][:, cols], bank[:])
+
+        def empty(name, blk, half):
+            if (name, blk) not in rows:
+                if name == "g":
+                    rows[name, blk] = lap.tile([P, S], F32, name="rows_g%d" % blk, offset=blk * T)
+                else:
+                    rows[name, blk] = sb.tile([P, S], F32, name="rows_%s%d" % (name, blk))
+            nc.scalar.copy(rows[name, blk][:, half * BANK : (half + 1) * BANK], banks[name, blk, half][:])
 
         at_cen = {}
 
         def centre(name, blk):
-            at_cen[name, blk] = sb.tile([P, V], F32, name="cen_%s%d" % (name, blk))
+            if (name, blk) == ("g", 0):
+                at_cen[name, blk] = lap.tile([P, V], F32, name="cen_g0", offset=2 * T)
+            else:
+                at_cen[name, blk] = sb.tile([P, V], F32, name="cen_%s%d" % (name, blk))
             nc.vector.tensor_copy(at_cen[name, blk][:], rows[name, blk][:].indirect(lists["cen"][:]))
 
         def scaled(blk, d, c0, c1):
@@ -141,40 +163,33 @@ def tile_picked_filmg_relu_p_kernel(
         vcopy, scopy = nc.vector.tensor_copy, nc.scalar.copy
         H = V // 2
 
+        for blk in range(2):
+            cast("g", blk, scopy)
+            quantize("g", blk)
         pick_words(0)
-        cast("g", 0, scopy)
         pick_words(1)
-        quantize("g", 0)
-        cast("g", 1, scopy)
-        cast("s", 0, scopy)
-        product("g", 0, 0, 0, scopy)
-        quantize("g", 1)
-        cast("s", 1, vcopy)
-        quantize("s", 0)
-        cast("h", 0, vcopy)
-        product("g", 0, 1, 1, vcopy)
-        quantize("s", 1)
-        quantize("h", 0)
-        product("s", 0, 0, 2, scopy)
-        product("s", 0, 1, 3, scopy)
+        for name, copy in (("s", scopy), ("h", vcopy)):
+            for blk in range(2):
+                cast(name, blk, copy)
+            for blk in range(2):
+                quantize(name, blk)
+        order = (
+            ("g", 0, 0, 0), ("g", 0, 1, 2), ("s", 0, 0, 3), ("s", 0, 1, 4), ("h", 0, 0, 5), ("h", 0, 1, 6),
+            ("g", 1, 0, 1), ("g", 1, 1, 5), ("s", 1, 0, 3), ("s", 1, 1, 4), ("h", 1, 0, 7), ("h", 1, 1, 0),
+        )
+        for name, blk, half, b in order:
+            if (name, blk, half) != ("g", 1, 0):
+                product(name, blk, half, b)
+            if (name, blk, half) == ("g", 0, 0):
+                product("g", 1, 0, 1)
+            empty(name, blk, half)
         centre("g", 0)
-        product("h", 0, 0, 4, scopy)
-        product("h", 0, 1, 5, scopy)
         centre("s", 0)
-        cast("h", 1, scopy)
-        product("g", 1, 0, 6, scopy)
-        product("g", 1, 1, 7, scopy)
-        quantize("h", 1)
-        product("s", 1, 0, 0, scopy)
-        product("s", 1, 1, 1, scopy)
 
-        acc0 = bank_tile(7)
-        for d in range(3):
-            if d == 2:
-                product("h", 1, 0, 2, scopy)
-                product("h", 1, 1, 3, scopy)
+        acc0 = bank_tile(3)
+        for d, b in enumerate((2, 1, 6)):
             u = scaled(0, d, 0, V)
-            z = bank_tile(4 + d)
+            z = bank_tile(b)
             turn(z, at_cen["s", 0], V, True, False)
             turn(z, u, V, False, True)
             r = relu_of(z, "r0%d" % d)
@@ -191,15 +206,15 @@ def tile_picked_filmg_relu_p_kernel(
         turn(z, shift, V, True, False)
         turn(z, u, V, False, True)
         r10 = relu_of(z, "r10")
-        z = bank_tile(7)
+        z = bank_tile(3)
         turn(z[:, 0:H], shift, H, True, False)
         turn(z[:, H:V], shift, H, False, False)
         for d in (1, 2):
             u = scaled(1, d, 0, H)
             turn(z[:, (d - 1) * H : d * H], u, H, False, d == 2)
-        acc_b = bank_tile(0)
+        acc_b = bank_tile(7)
         turn(acc_b, r10[:, H:V], H, True, True)
-        acc_a = bank_tile(1)
+        acc_a = bank_tile(0)
         turn(acc_a, r10[:, 0:H], H, True, False)
         r = relu_of(z, "r1a")
         turn(acc_a, r[:, 0:H], H, False, False)

@@ -38,7 +38,7 @@ def tile_picked_filmg_relu_p_kernel(
             return ps.tile([P, BANK], F32, name="bank%d" % b)
 
         first = P - SCALE_ROWS
-        scale_table = lap.tile([P, T], U8, name="scale_table", offset=T // 2 + 32)
+        scale_table = sb.tile([P, T], U8, name="scale_table")
         nc.sync.dma_start(out=scale_table[first:P, :].bitcast(I32), in_=x_scales[0].bitcast(I32))
         lists = {}
 
@@ -48,17 +48,17 @@ def tile_picked_filmg_relu_p_kernel(
 
         raw = {}
 
-        def load_weights(name, src, dst):
-            nc.sync.dma_start(out=dst[:], in_=src.rearrange("(p j) n -> p j n", j=PACK))
-            for blk in range(2):
-                raw[name, blk] = dst[:, :, blk * P : (blk + 1) * P]
+        def load_half(name, src, blk, dst):
+            nc.sync.dma_start(out=dst[:], in_=src.rearrange("(p j) n -> p j n", j=PACK)[:, :, blk * P : (blk + 1) * P])
+            raw[name, blk] = dst[:]
 
         load_list("offs", offs)
-        load_weights("g", w1, sb.tile([P, PACK, N], F32, name="raw_g"))
+        load_half("g", w1, 0, lap.tile([P, PACK, P], F32, name="raw_g0", offset=10240))
         for name, src in (("cen", cen), ("pos1", pos1), ("pos2", pos2)):
             load_list(name, src)
         word_table = sb.tile([P, T], I32, name="word_table", align_bytes=64)
         nc.sync.dma_start(out=word_table[:], in_=x_words[0].rearrange("p n t -> p (n t)").bitcast(I32))
+        load_half("s", w2, 0, lap.tile([P, PACK, P], F32, name="raw_s0", offset=6176))
         load_list("pos3", pos3)
 
         nc.vector.memset(scale_table[0:first, :].bitcast(I32), 0)
@@ -76,8 +76,6 @@ def tile_picked_filmg_relu_p_kernel(
                 out=x_plane[32 * q : 32 * q + 4, :].bitcast(I32),
                 in_=picked_scales[first + 4 * q : first + 4 * q + 4, :].bitcast(I32),
             )
-        load_weights("s", w2, lap.tile([P, PACK, N], F32, name="raw_s", offset=32))
-        load_weights("h", w3, lap.tile([P, PACK, N], F32, name="raw_h", offset=T + 32))
 
         x_codes = []
 
@@ -90,16 +88,29 @@ def tile_picked_filmg_relu_p_kernel(
             x_codes.append(codes)
 
         grouped, w_codes, w_plane, rows = {}, {}, {}, {}
+        group_at = {("g", 0): 16384}
+        codes_at = {("s", 1): 20480, ("g", 1): 22528, ("h", 1): 24576}
+        relu_at = {"r00": 20480, "r01": 22528, "r02": 24576, "r10": 24576}
 
         def cast(name, blk, engine_copy):
-            grouped[name, blk] = sb.tile([P, P, PACK], BF16, name="grp_%s%d" % (name, blk), align_bytes=64)
+            if (name, blk) in group_at:
+                grouped[name, blk] = lap.tile(
+                    [P, P, PACK], BF16, name="grp_%s%d" % (name, blk), align_bytes=64, offset=group_at[name, blk]
+                )
+            else:
+                grouped[name, blk] = sb.tile([P, P, PACK], BF16, name="grp_%s%d" % (name, blk), align_bytes=64)
             engine_copy(
                 grouped[name, blk][:].rearrange("p (c i) t -> p c t i", i=4),
                 raw[name, blk].rearrange("p t (c i) -> p c t i", i=4),
             )
 
         def quantize(name, blk):
-            w_codes[name, blk] = sb.tile([P, P], U32, name="wc_%s%d" % (name, blk), align_bytes=64)
+            if (name, blk) in codes_at:
+                w_codes[name, blk] = lap.tile(
+                    [P, P], U32, name="wc_%s%d" % (name, blk), align_bytes=64, offset=codes_at[name, blk]
+                )
+            else:
+                w_codes[name, blk] = sb.tile([P, P], U32, name="wc_%s%d" % (name, blk), align_bytes=64)
             w_plane[name, blk] = sb.tile([P, P], U8, name="wp_%s%d" % (name, blk), align_bytes=64)
             nc.vector.quantize_mx(
                 out=w_codes[name, blk][:].bitcast(FP8X4),
@@ -109,31 +120,34 @@ def tile_picked_filmg_relu_p_kernel(
 
         banks = {}
 
-        def product(name, blk, half, b):
-            banks[name, blk, half] = bank_tile(b)
+        def product(name, blk, c0, n, b):
+            banks[name, blk, c0] = (bank_tile(b), n)
+            half, at = divmod(c0, BANK)
             nc.tensor.matmul_mx(
-                out=banks[name, blk, half][:],
+                out=banks[name, blk, c0][0][:, 0:n],
                 lhsT=w_codes[name, blk][:].bitcast(FP8X4),
                 lhsT_scale=w_plane[name, blk][:],
-                rhs=x_codes[half][:].bitcast(FP8X4),
-                rhs_scale=x_plane[:, half * BANK : (half + 1) * BANK],
+                rhs=x_codes[half][:, at : at + n].bitcast(FP8X4),
+                rhs_scale=x_plane[:, c0 : c0 + n],
                 start=True,
                 stop=True,
             )
 
-        def empty(name, blk, half):
+        def empty(name, blk, c0):
             if (name, blk) not in rows:
-                if name == "g":
-                    rows[name, blk] = lap.tile([P, S], F32, name="rows_g%d" % blk, offset=blk * T)
+                if (name, blk) == ("g", 0):
+                    rows[name, blk] = lap.tile([P, S], F32, name="rows_g0", offset=6176)
                 else:
                     rows[name, blk] = sb.tile([P, S], F32, name="rows_%s%d" % (name, blk))
-            nc.scalar.copy(rows[name, blk][:, half * BANK : (half + 1) * BANK], banks[name, blk, half][:])
+            bank, n = banks[name, blk, c0]
+            nc.scalar.copy(rows[name, blk][:, c0 : c0 + n], bank[:, 0:n])
 
         at_cen = {}
+        cen_at = {("g", 0): 14368, ("s", 0): 17408}
 
         def centre(name, blk):
-            if (name, blk) == ("g", 0):
-                at_cen[name, blk] = lap.tile([P, V], F32, name="cen_g0", offset=2 * T)
+            if (name, blk) in cen_at:
+                at_cen[name, blk] = lap.tile([P, V], F32, name="cen_%s%d" % (name, blk), offset=cen_at[name, blk])
             else:
                 at_cen[name, blk] = sb.tile([P, V], F32, name="cen_%s%d" % (name, blk))
             nc.vector.tensor_copy(at_cen[name, blk][:], rows[name, blk][:].indirect(lists["cen"][:]))
@@ -155,82 +169,106 @@ def tile_picked_filmg_relu_p_kernel(
                     stop=stop and j == n // P - 1,
                 )
 
-        def relu_of(z, name):
-            r = sb.tile([P, BANK], F32, name=name)
-            nc.scalar.activation(r[:], z[:], RELU)
+        def relu_of(z, name, c0=0, c1=BANK):
+            if name in relu_at:
+                r = lap.tile([P, c1 - c0], F32, name=name, offset=relu_at[name])
+            else:
+                r = sb.tile([P, c1 - c0], F32, name=name)
+            nc.scalar.activation(r[:], z[:, c0:c1], RELU)
             return r
 
         vcopy, scopy = nc.vector.tensor_copy, nc.scalar.copy
         H = V // 2
 
-        for blk in range(2):
-            cast("g", blk, scopy)
-            quantize("g", blk)
+        cast("g", 0, scopy)
+        load_half("h", w3, 0, lap.tile([P, PACK, P], F32, name="raw_h0", offset=8224))
+        load_half("s", w2, 1, lap.tile([P, PACK, P], F32, name="raw_s1", offset=12256))
+        quantize("g", 0)
+        load_half("g", w1, 1, lap.tile([P, PACK, P], F32, name="raw_g1", offset=14368))
+        load_half("h", w3, 1, lap.tile([P, PACK, P], F32, name="raw_h1", offset=17376))
         pick_words(0)
         pick_words(1)
-        for name, copy in (("s", scopy), ("h", vcopy)):
-            for blk in range(2):
-                cast(name, blk, copy)
-            for blk in range(2):
-                quantize(name, blk)
-        order = (
-            ("g", 0, 0, 0), ("g", 0, 1, 2), ("s", 0, 0, 3), ("s", 0, 1, 4), ("h", 0, 0, 5), ("h", 0, 1, 6),
-            ("g", 1, 0, 1), ("g", 1, 1, 5), ("s", 1, 0, 3), ("s", 1, 1, 4), ("h", 1, 0, 7), ("h", 1, 1, 0),
-        )
-        for name, blk, half, b in order:
-            if (name, blk, half) != ("g", 1, 0):
-                product(name, blk, half, b)
-            if (name, blk, half) == ("g", 0, 0):
-                product("g", 1, 0, 1)
-            empty(name, blk, half)
+        cast("s", 0, scopy)
+        cast("h", 0, scopy)
+        product("g", 0, 0, BANK, 0)
+        product("g", 0, BANK, H, 1)
+        product("g", 0, BANK + H, H, 2)
+        quantize("s", 0)
+        quantize("h", 0)
+        cast("s", 1, vcopy)
+        cast("g", 1, vcopy)
+        quantize("s", 1)
+        quantize("g", 1)
+        for c0 in (0, BANK, BANK + H):
+            empty("g", 0, c0)
+        for name, bs in (("s", (0, 1)), ("h", (2, 0))):
+            for half in range(2):
+                product(name, 0, half * BANK, BANK, bs[half])
+                empty(name, 0, half * BANK)
         centre("g", 0)
+        cast("h", 1, vcopy)
         centre("s", 0)
+        quantize("h", 1)
+        for half in range(2):
+            product("s", 1, half * BANK, BANK, 1 + half)
+            empty("s", 1, half * BANK)
+        product("g", 1, 0, BANK, 0)
+        empty("g", 1, 0)
 
-        acc0 = bank_tile(3)
-        for d, b in enumerate((2, 1, 6)):
-            u = scaled(0, d, 0, V)
-            z = bank_tile(b)
-            turn(z, at_cen["s", 0], V, True, False)
-            turn(z, u, V, False, True)
-            r = relu_of(z, "r0%d" % d)
-            turn(acc0, r, V, d == 0, d == 2)
+        shift = at_cen["s", 0]
+        z0 = bank_tile(3)
+        turn(z0, shift, V, True, False)
+        product("g", 1, BANK, BANK, 1)
+        u = scaled(0, 0, 0, V)
+        turn(z0, u, V, False, True)
+        product("h", 1, 0, BANK, 2)
+        r = relu_of(z0, "r00")
+        empty("g", 1, BANK)
+        empty("h", 1, 0)
+        z1 = bank_tile(4)
+        turn(z1, shift, V, True, False)
+        product("h", 1, BANK, BANK, 0)
+        u = scaled(0, 1, 0, V)
+        turn(z1, u, V, False, True)
+        acc0 = bank_tile(5)
+        turn(acc0, r, V, True, False)
+        r = relu_of(z1, "r01")
+        empty("h", 1, BANK)
+        z2 = bank_tile(1)
+        turn(z2, shift, V, True, False)
+        u = scaled(0, 2, 0, V)
+        turn(z2, u, V, False, True)
+        turn(acc0, r, V, False, False)
+        r = relu_of(z2, "r02")
+        turn(acc0, r, V, False, True)
+        centre("s", 1)
+        centre("g", 1)
         res0 = sb.tile([P, V], F32, name="res0")
         nc.scalar.copy(res0[:], acc0[:])
         nc.scalar.dma_start(out=out[0:P, :], in_=res0[:])
 
-        centre("g", 1)
-        centre("s", 1)
         shift = at_cen["s", 1]
+        zs = [bank_tile(b) for b in (1, 4)]
+        for z in zs:
+            turn(z, shift, V, True, False)
         u = scaled(1, 0, 0, V)
-        z = bank_tile(6)
-        turn(z, shift, V, True, False)
-        turn(z, u, V, False, True)
-        r10 = relu_of(z, "r10")
-        z = bank_tile(3)
-        turn(z[:, 0:H], shift, H, True, False)
-        turn(z[:, H:V], shift, H, False, False)
-        for d in (1, 2):
-            u = scaled(1, d, 0, H)
-            turn(z[:, (d - 1) * H : d * H], u, H, False, d == 2)
-        acc_b = bank_tile(7)
-        turn(acc_b, r10[:, H:V], H, True, True)
-        acc_a = bank_tile(0)
-        turn(acc_a, r10[:, 0:H], H, True, False)
-        r = relu_of(z, "r1a")
-        turn(acc_a, r[:, 0:H], H, False, False)
-        turn(acc_a, r[:, H:V], H, False, True)
-        res_a = sb.tile([P, H], F32, name="res_a")
-        nc.scalar.copy(res_a[:], acc_a[:, 0:H])
-        nc.scalar.dma_start(out=out[P : 2 * P, 0:H], in_=res_a[:])
-
-        us = [scaled(1, d, H, V) for d in (1, 2)]
-        zs = []
-        for d, u in enumerate(us):
-            z = sb.tile([P, H], F32, name="z_tail%d" % d)
-            nc.vector.tensor_tensor(z[:], u[:], shift[:, H:V], ADD)
-            zs.append(z)
-        part = sb.tile([P, H], F32, name="part")
-        nc.vector.scalar_tensor_tensor(part[:], zs[0][:], 0.0, acc_b[:, 0:H], MAX, ADD)
-        res_b = sb.tile([P, H], F32, name="res_b")
-        nc.vector.scalar_tensor_tensor(res_b[:], zs[1][:], 0.0, part[:], MAX, ADD)
-        nc.sync.dma_start(out=out[P : 2 * P, H:V], in_=res_b[:])
+        turn(zs[0], u, V, False, True)
+        r10 = relu_of(zs[0], "r10")
+        accs = [bank_tile(b) for b in (6, 7)]
+        u = scaled(1, 1, 0, V)
+        for a in range(2):
+            turn(accs[a], r10[:, a * H : (a + 1) * H], H, True, False)
+        turn(zs[1], u, V, False, True)
+        for a in range(2):
+            r = relu_of(zs[1], "r11_%d" % a, a * H, (a + 1) * H)
+            turn(accs[a], r, H, False, True)
+        us = [scaled(1, 2, a * H, (a + 1) * H) for a in range(2)]
+        zt = []
+        for a in range(2):
+            z = sb.tile([P, H], F32, name="z_tail%d" % a)
+            nc.vector.tensor_tensor(z[:], us[a][:], shift[:, a * H : (a + 1) * H], ADD)
+            zt.append(z)
+        for a in range(2):
+            res = sb.tile([P, H], F32, name="res1_%d" % a)
+            nc.vector.scalar_tensor_tensor(res[:], zt[a][:], 0.0, accs[a][:, 0:H], MAX, ADD)
+            nc.sync.dma_start(out=out[P : 2 * P, a * H : (a + 1) * H], in_=res[:])

@@ -89,7 +89,7 @@ def tile_picked_filmg_relu_p_kernel(
 
         grouped, w_codes, w_plane, rows = {}, {}, {}, {}
         group_at = {("g", 0): 16384}
-        codes_at = {("s", 1): 20480, ("g", 1): 22528, ("h", 1): 24576}
+        codes_at = {("g", 1): 20480, ("s", 1): 22528, ("h", 1): 24576}
         relu_at = {"r00": 20480, "r01": 22528, "r02": 24576, "r10": 24576}
 
         def cast(name, blk, engine_copy):
@@ -210,20 +210,20 @@ def tile_picked_filmg_relu_p_kernel(
         centre("s", 0)
         quantize("h", 1)
         for half in range(2):
-            product("s", 1, half * BANK, BANK, 1 + half)
-            empty("s", 1, half * BANK)
-        product("g", 1, 0, BANK, 0)
-        empty("g", 1, 0)
+            product("g", 1, half * BANK, BANK, 1 + half)
+            empty("g", 1, half * BANK)
+        product("s", 1, 0, BANK, 0)
+        empty("s", 1, 0)
 
         shift = at_cen["s", 0]
         z0 = bank_tile(3)
         turn(z0, shift, V, True, False)
-        product("g", 1, BANK, BANK, 1)
+        product("s", 1, BANK, BANK, 1)
         u = scaled(0, 0, 0, V)
         turn(z0, u, V, False, True)
         product("h", 1, 0, BANK, 2)
         r = relu_of(z0, "r00")
-        empty("g", 1, BANK)
+        empty("s", 1, BANK)
         empty("h", 1, 0)
         z1 = bank_tile(4)
         turn(z1, shift, V, True, False)
@@ -241,26 +241,28 @@ def tile_picked_filmg_relu_p_kernel(
         turn(acc0, r, V, False, False)
         r = relu_of(z2, "r02")
         turn(acc0, r, V, False, True)
-        centre("s", 1)
         centre("g", 1)
+        centre("s", 1)
         res0 = sb.tile([P, V], F32, name="res0")
         nc.scalar.copy(res0[:], acc0[:])
         nc.scalar.dma_start(out=out[0:P, :], in_=res0[:])
 
         shift = at_cen["s", 1]
-        zs = [bank_tile(b) for b in (1, 4)]
-        for z in zs:
-            turn(z, shift, V, True, False)
+        z0 = bank_tile(1)
+        turn(z0, shift, V, True, False)
+        zs = [bank_tile(b) for b in (4, 3)]
+        for a in range(2):
+            turn(zs[a], shift[:, a * H : (a + 1) * H], H, True, False)
         u = scaled(1, 0, 0, V)
-        turn(zs[0], u, V, False, True)
-        r10 = relu_of(zs[0], "r10")
+        turn(z0, u, V, False, True)
+        r10 = relu_of(z0, "r10")
         accs = [bank_tile(b) for b in (6, 7)]
-        u = scaled(1, 1, 0, V)
         for a in range(2):
             turn(accs[a], r10[:, a * H : (a + 1) * H], H, True, False)
-        turn(zs[1], u, V, False, True)
         for a in range(2):
-            r = relu_of(zs[1], "r11_%d" % a, a * H, (a + 1) * H)
+            u = scaled(1, 1, a * H, (a + 1) * H)
+            turn(zs[a], u, H, False, True)
+            r = relu_of(zs[a], "r11_%d" % a, 0, H)
             turn(accs[a], r, H, False, True)
         us = [scaled(1, 2, a * H, (a + 1) * H) for a in range(2)]
         zt = []

@@ -52,13 +52,18 @@ def tile_picked_filmg_relu_p_kernel(
             nc.sync.dma_start(out=dst[:], in_=src.rearrange("(p j) n -> p j n", j=PACK)[:, :, blk * P : (blk + 1) * P])
             raw[name, blk] = dst[:]
 
+        def load_whole(name, src, dst):
+            nc.sync.dma_start(out=dst[:], in_=src.rearrange("(p j) n -> p j n", j=PACK))
+            for blk in range(2):
+                raw[name, blk] = dst[:, :, blk * P : (blk + 1) * P]
+
         load_list("offs", offs)
         load_half("g", w1, 0, lap.tile([P, PACK, P], F32, name="raw_g0", offset=10240))
         for name, src in (("cen", cen), ("pos1", pos1), ("pos2", pos2)):
             load_list(name, src)
         word_table = sb.tile([P, T], I32, name="word_table", align_bytes=64)
         nc.sync.dma_start(out=word_table[:], in_=x_words[0].rearrange("p n t -> p (n t)").bitcast(I32))
-        load_half("s", w2, 0, lap.tile([P, PACK, P], F32, name="raw_s0", offset=6176))
+        load_whole("s", w2, sb.tile([P, PACK, N], F32, name="raw_s"))
         load_list("pos3", pos3)
 
         nc.vector.memset(scale_table[0:first, :].bitcast(I32), 0)
@@ -88,7 +93,7 @@ def tile_picked_filmg_relu_p_kernel(
             x_codes.append(codes)
 
         grouped, w_codes, w_plane, rows = {}, {}, {}, {}
-        group_at = {("g", 0): 16384}
+        group_at = {}
         codes_at = {("g", 1): 20480, ("s", 1): 22528, ("h", 1): 24576}
         relu_at = {"r00": 20480, "r01": 22528, "r02": 24576, "r10": 24576}
 
@@ -135,15 +140,12 @@ def tile_picked_filmg_relu_p_kernel(
 
         def empty(name, blk, c0):
             if (name, blk) not in rows:
-                if (name, blk) == ("g", 0):
-                    rows[name, blk] = lap.tile([P, S], F32, name="rows_g0", offset=6176)
-                else:
-                    rows[name, blk] = sb.tile([P, S], F32, name="rows_%s%d" % (name, blk))
+                rows[name, blk] = sb.tile([P, S], F32, name="rows_%s%d" % (name, blk))
             bank, n = banks[name, blk, c0]
             nc.scalar.copy(rows[name, blk][:, c0 : c0 + n], bank[:, 0:n])
 
         at_cen = {}
-        cen_at = {("g", 0): 14368, ("s", 0): 17408}
+        cen_at = {("g", 0): 6176, ("s", 0): 12288}
 
         def centre(name, blk):
             if (name, blk) in cen_at:
@@ -181,24 +183,22 @@ def tile_picked_filmg_relu_p_kernel(
         H = V // 2
 
         cast("g", 0, scopy)
-        load_half("h", w3, 0, lap.tile([P, PACK, P], F32, name="raw_h0", offset=8224))
-        load_half("s", w2, 1, lap.tile([P, PACK, P], F32, name="raw_s1", offset=12256))
+        load_whole("h", w3, lap.tile([P, PACK, N], F32, name="raw_h", offset=6176))
+        load_half("g", w1, 1, lap.tile([P, PACK, P], F32, name="raw_g1", offset=12256))
         quantize("g", 0)
-        load_half("g", w1, 1, lap.tile([P, PACK, P], F32, name="raw_g1", offset=14368))
-        load_half("h", w3, 1, lap.tile([P, PACK, P], F32, name="raw_h1", offset=17376))
         pick_words(0)
         pick_words(1)
         cast("s", 0, scopy)
-        cast("h", 0, scopy)
         product("g", 0, 0, BANK, 0)
         product("g", 0, BANK, H, 1)
         product("g", 0, BANK + H, H, 2)
-        quantize("s", 0)
-        quantize("h", 0)
         cast("s", 1, vcopy)
-        cast("g", 1, vcopy)
-        quantize("s", 1)
-        quantize("g", 1)
+        for blk in range(2):
+            quantize("s", blk)
+        for blk in range(2):
+            cast("h", blk, vcopy)
+        for blk in range(2):
+            quantize("h", blk)
         for c0 in (0, BANK, BANK + H):
             empty("g", 0, c0)
         for name, bs in (("s", (0, 1)), ("h", (2, 0))):
@@ -206,9 +206,9 @@ def tile_picked_filmg_relu_p_kernel(
                 product(name, 0, half * BANK, BANK, bs[half])
                 empty(name, 0, half * BANK)
         centre("g", 0)
-        cast("h", 1, vcopy)
+        cast("g", 1, vcopy)
         centre("s", 0)
-        quantize("h", 1)
+        quantize("g", 1)
         for half in range(2):
             product("g", 1, half * BANK, BANK, 1 + half)
             empty("g", 1, half * BANK)

@@ -95,7 +95,7 @@ def tile_picked_filmg_relu_p_kernel(
         grouped, w_codes, w_plane, rows = {}, {}, {}, {}
         group_at = {}
         codes_at = {("g", 1): 20480, ("s", 1): 22528, ("h", 1): 24576}
-        relu_at = {"r00": 20480, "r01": 22528, "r02": 24576, "r10": 24576}
+        relu_at = {"r00": 20480, "r01": 22528, "r02": 24576, "r10_0": 24576}
 
         def cast(name, blk, engine_copy):
             if (name, blk) in group_at:
@@ -248,22 +248,18 @@ def tile_picked_filmg_relu_p_kernel(
         nc.scalar.dma_start(out=out[0:P, :], in_=res0[:])
 
         shift = at_cen["s", 1]
-        z0 = bank_tile(1)
-        turn(z0, shift, V, True, False)
-        zs = [bank_tile(b) for b in (4, 3)]
-        for a in range(2):
-            turn(zs[a], shift[:, a * H : (a + 1) * H], H, True, False)
-        u = scaled(1, 0, 0, V)
-        turn(z0, u, V, False, True)
-        r10 = relu_of(z0, "r10")
+        zs = {}
+        for (a, d), b in zip(((0, 0), (0, 1), (1, 0), (1, 1)), (1, 4, 3, 0)):
+            zs[a, d] = bank_tile(b)
+            turn(zs[a, d], shift[:, a * H : (a + 1) * H], H, True, False)
         accs = [bank_tile(b) for b in (6, 7)]
         for a in range(2):
-            turn(accs[a], r10[:, a * H : (a + 1) * H], H, True, False)
-        for a in range(2):
-            u = scaled(1, 1, a * H, (a + 1) * H)
-            turn(zs[a], u, H, False, True)
-            r = relu_of(zs[a], "r11_%d" % a, 0, H)
-            turn(accs[a], r, H, False, True)
+            for d in range(2):
+                u = scaled(1, d, a * H, (a + 1) * H)
+                turn(zs[a, d], u, H, False, True)
+            for d in range(2):
+                r = relu_of(zs[a, d], "r1%d_%d" % (d, a), 0, H)
+                turn(accs[a], r, H, d == 0, d == 1)
         us = [scaled(1, 2, a * H, (a + 1) * H) for a in range(2)]
         zt = []
         for a in range(2):

@@ -188,11 +188,21 @@ def tile_picked_filmg_relu_p_kernel(
         quantize("g", 0)
         pick_words(0)
         pick_words(1)
-        cast("s", 0, scopy)
+        for blk in range(2):
+            cast("s", blk, scopy)
         product("g", 0, 0, BANK, 0)
+        spare = bank_tile(7)
+        nc.tensor.matmul_mx(
+            out=spare[:],
+            lhsT=w_codes["g", 0][:].bitcast(FP8X4),
+            lhsT_scale=w_plane["g", 0][:],
+            rhs=x_codes[0][:].bitcast(FP8X4),
+            rhs_scale=x_plane[:, 0:BANK],
+            start=True,
+            stop=True,
+        )
         product("g", 0, BANK, H, 1)
         product("g", 0, BANK + H, H, 2)
-        cast("s", 1, vcopy)
         for blk in range(2):
             quantize("s", blk)
         for blk in range(2):

@@ -191,16 +191,6 @@ def tile_picked_filmg_relu_p_kernel(
         for blk in range(2):
             cast("s", blk, scopy)
         product("g", 0, 0, BANK, 0)
-        spare = bank_tile(7)
-        nc.tensor.matmul_mx(
-            out=spare[:],
-            lhsT=w_codes["g", 0][:].bitcast(FP8X4),
-            lhsT_scale=w_plane["g", 0][:],
-            rhs=x_codes[0][:].bitcast(FP8X4),
-            rhs_scale=x_plane[:, 0:BANK],
-            start=True,
-            stop=True,
-        )
         product("g", 0, BANK, H, 1)
         product("g", 0, BANK + H, H, 2)
         for blk in range(2):

@@ -14,6 +14,7 @@ U16 = mybir.dt.uint16
 U8 = mybir.dt.uint8
 FP8X4 = mybir.dt.float8_e4m3fn_x4
 RELU = mybir.ActivationFunctionType.Relu
+COPY = mybir.ActivationFunctionType.Copy
 MULT = mybir.AluOpType.mult
 ADD = mybir.AluOpType.add
 MAX = mybir.AluOpType.max
@@ -23,6 +24,7 @@ PACK = 4
 BANK = 512
 SCALE_ROWS = 16
 LIST_GROUP = 16
+HALF = V // 2
 
 
 def tile_picked_filmg_relu_p_kernel(
@@ -33,37 +35,156 @@ def tile_picked_filmg_relu_p_kernel(
         sb = ctx.enter_context(tc.tile_pool(name="sb", bufs=1))
         lap = ctx.enter_context(tc.tile_pool(name="lap", bufs=1))
         ps = ctx.enter_context(tc.psum_pool(name="ps", bufs=1))
+        vcopy, scopy = nc.vector.tensor_copy, nc.scalar.copy
+        lists, raw, grouped, w_codes, w_plane, banks, rows, at_cen, x_codes = {}, {}, {}, {}, {}, {}, {}, {}, {}
+        place = {}
+
+        def tile(shape, dtype, name, **kw):
+            if name in place:
+                return lap.tile(shape, dtype, name=name, offset=place[name], **kw)
+            return sb.tile(shape, dtype, name=name, **kw)
+
+        psum = [ps.tile([P, BANK], F32, name="bank%d" % b) for b in range(8)]
 
         def bank_tile(b):
-            return ps.tile([P, BANK], F32, name="bank%d" % b)
-
-        first = P - SCALE_ROWS
-        scale_table = sb.tile([P, T], U8, name="scale_table")
-        nc.sync.dma_start(out=scale_table[first:P, :].bitcast(I32), in_=x_scales[0].bitcast(I32))
-        lists = {}
+            return psum[b]
 
         def load_list(name, src):
             lists[name] = sb.tile(list(src.shape), U16, name="list_" + name)
             nc.sync.dma_start(lists[name][:], src)
 
-        raw = {}
+        def offsets(name, c0, c1):
+            return lists[name][:, c0 // LIST_GROUP : c1 // LIST_GROUP]
 
-        def load_half(name, src, blk, dst):
-            nc.sync.dma_start(out=dst[:], in_=src.rearrange("(p j) n -> p j n", j=PACK)[:, :, blk * P : (blk + 1) * P])
+        def load_half(name, src, blk, queue=nc.sync):
+            dst = tile([P, PACK, P], F32, "raw_%s%d" % (name, blk))
+            queue.dma_start(out=dst[:], in_=src.rearrange("(p j) n -> p j n", j=PACK)[:, :, blk * P : (blk + 1) * P])
             raw[name, blk] = dst[:]
 
-        def load_whole(name, src, dst):
-            nc.sync.dma_start(out=dst[:], in_=src.rearrange("(p j) n -> p j n", j=PACK))
+        def load_whole(name, src, queue=nc.sync):
+            dst = tile([P, PACK, N], F32, "raw_" + name)
+            queue.dma_start(out=dst[:], in_=src.rearrange("(p j) n -> p j n", j=PACK))
+            raw[name] = dst[:]
             for blk in range(2):
                 raw[name, blk] = dst[:, :, blk * P : (blk + 1) * P]
 
+        def gcopy(dst, src):
+            nc.gpsimd.tensor_scalar(dst, src, 1.0, 0.0, MULT, ADD)
+
+        def cast(name, blk, engine_copy):
+            grouped[name, blk] = tile([P, P, PACK], BF16, "grp_%s%d" % (name, blk), align_bytes=64)
+            engine_copy(
+                grouped[name, blk][:].rearrange("p (c i) t -> p c t i", i=4),
+                raw[name, blk].rearrange("p t (c i) -> p c t i", i=4),
+            )
+
+        def quantize(name, blk):
+            w_codes[name, blk] = tile([P, P], U32, "wc_%s%d" % (name, blk), align_bytes=64)[:]
+            w_plane[name, blk] = tile([P, P], U8, "wp_%s%d" % (name, blk), align_bytes=64)[:]
+            nc.vector.quantize_mx(
+                out=w_codes[name, blk].bitcast(FP8X4),
+                scales=w_plane[name, blk],
+                in_=grouped[name, blk][:].rearrange("p c t -> p (c t)"),
+            )
+
+        def cast_whole(name, engine_copy):
+            grouped[name] = tile([P, N, PACK], BF16, "grp_" + name, align_bytes=64)
+            engine_copy(
+                grouped[name][:].rearrange("p (c i) t -> p c t i", i=4),
+                raw[name].rearrange("p t (c i) -> p c t i", i=4),
+            )
+
+        def quantize_whole(name):
+            codes = tile([P, N], U32, "wc_" + name, align_bytes=64)
+            plane = tile([P, N], U8, "wp_" + name, align_bytes=64)
+            nc.vector.quantize_mx(
+                out=codes[:].bitcast(FP8X4), scales=plane[:], in_=grouped[name][:].rearrange("p c t -> p (c t)")
+            )
+            for blk in range(2):
+                w_codes[name, blk] = codes[:, blk * P : (blk + 1) * P]
+                w_plane[name, blk] = plane[:, blk * P : (blk + 1) * P]
+
+        def pick_words(half):
+            x_codes[half] = tile([P, BANK], U32, "x_codes%d" % half, align_bytes=64)
+            nc.vector.tensor_copy(
+                x_codes[half][:], word_table[:].bitcast(U32).indirect(offsets("offs", half * BANK, (half + 1) * BANK))
+            )
+
+        def product(name, blk, c0, b, n=BANK):
+            banks[name, blk, c0] = (bank_tile(b), n)
+            half, at = divmod(c0, BANK)
+            nc.tensor.matmul_mx(
+                out=banks[name, blk, c0][0][:, 0:n],
+                lhsT=w_codes[name, blk].bitcast(FP8X4),
+                lhsT_scale=w_plane[name, blk],
+                rhs=x_codes[half][:, at : at + n].bitcast(FP8X4),
+                rhs_scale=x_plane[:, c0 : c0 + n],
+                start=True,
+                stop=True,
+            )
+
+        def empty(name, blk, c0, engine_copy):
+            if (name, blk) not in rows:
+                rows[name, blk] = tile([P, S], F32, "rows_%s%d" % (name, blk))
+            bank, n = banks[name, blk, c0]
+            engine_copy(rows[name, blk][:, c0 : c0 + n], bank[:, 0:n])
+
+        def centre(name, blk, c0=0, c1=V, on_vector=False):
+            if (name, blk) not in at_cen:
+                at_cen[name, blk] = tile([P, V], F32, "cen_%s%d" % (name, blk))
+            picked = rows[name, blk][:].indirect(offsets("cen", c0, c1))
+            if on_vector:
+                nc.vector.tensor_copy(at_cen[name, blk][:, c0:c1], picked)
+            else:
+                nc.scalar.activation(at_cen[name, blk][:, c0:c1], picked, COPY)
+
+        def scaled(blk, d, c0=0, c1=V):
+            u = tile([P, c1 - c0], F32, "u_%d_%d_%d" % (blk, d, c0))
+            picked = rows["h", blk][:].indirect(offsets("pos%d" % (d + 1), c0, c1))
+            nc.vector.tensor_tensor(u[:], picked, at_cen["g", blk][:, c0:c1], MULT)
+            return u
+
+        def turn(bank, src, start, stop):
+            n = src.shape[1]
+            for j in range(n // P):
+                nc.tensor.matmul(
+                    bank[:, j * P : (j + 1) * P],
+                    lhsT=src[:, j * P : (j + 1) * P],
+                    rhs=ident[:],
+                    is_transpose=True,
+                    start=start and j == 0,
+                    stop=stop and j == n // P - 1,
+                )
+
+        def relu_of(z, name):
+            r = tile([P, z.shape[1]], F32, name)
+            nc.scalar.activation(r[:], z, RELU)
+            return r
+
+        def shifted(u, blk, c0, name, engine=nc.vector):
+            n = u.shape[1]
+            z = tile([P, n], F32, name)
+            engine.tensor_tensor(z[:], u, at_cen["s", blk][:, c0 : c0 + n], ADD)
+            return z
+
+        def finish(z, acc, blk, c0, queue):
+            n = z.shape[1]
+            res = tile([P, n], F32, "res_%d_%d" % (blk, c0))
+            nc.vector.scalar_tensor_tensor(res[:], z, 0.0, acc, MAX, ADD)
+            queue.dma_start(out=out[blk * P : (blk + 1) * P, c0 : c0 + n], in_=res[:])
+
+        place.update({"raw_g0": 3072, "raw_s": 0, "raw_g1": 4096, "grp_h1": 5056, "u_0_0_0": 6112})
+        place.update({"grp_s": 8192, "rows_h0": 8192, "wc_g1": 12288, "cen_s0": 12288})
+        first = P - SCALE_ROWS
+        scale_table = sb.tile([P, T], U8, name="scale_table")
+        nc.sync.dma_start(out=scale_table[first:P, :].bitcast(I32), in_=x_scales[0].bitcast(I32))
         load_list("offs", offs)
-        load_half("g", w1, 0, lap.tile([P, PACK, P], F32, name="raw_g0", offset=10240))
+        load_half("g", w1, 0)
         for name, src in (("cen", cen), ("pos1", pos1), ("pos2", pos2)):
             load_list(name, src)
         word_table = sb.tile([P, T], I32, name="word_table", align_bytes=64)
         nc.sync.dma_start(out=word_table[:], in_=x_words[0].rearrange("p n t -> p (n t)").bitcast(I32))
-        load_whole("s", w2, sb.tile([P, PACK, N], F32, name="raw_s"))
+        load_whole("h", w3)
         load_list("pos3", pos3)
 
         nc.vector.memset(scale_table[0:first, :].bitcast(I32), 0)
@@ -81,192 +202,80 @@ def tile_picked_filmg_relu_p_kernel(
                 out=x_plane[32 * q : 32 * q + 4, :].bitcast(I32),
                 in_=picked_scales[first + 4 * q : first + 4 * q + 4, :].bitcast(I32),
             )
-
-        x_codes = []
-
-        def pick_words(half):
-            codes = sb.tile([P, BANK], U32, name="x_codes%d" % half, align_bytes=64)
-            cols = BANK // LIST_GROUP
-            nc.vector.tensor_copy(
-                codes[:], word_table[:].bitcast(U32).indirect(lists["offs"][:, half * cols : (half + 1) * cols])
-            )
-            x_codes.append(codes)
-
-        grouped, w_codes, w_plane, rows = {}, {}, {}, {}
-        group_at = {}
-        codes_at = {("g", 1): 20480, ("s", 1): 22528, ("h", 1): 24576}
-        relu_at = {"r00": 20480, "r01": 22528, "r02": 24576, "r10_0": 24576}
-
-        def cast(name, blk, engine_copy):
-            if (name, blk) in group_at:
-                grouped[name, blk] = lap.tile(
-                    [P, P, PACK], BF16, name="grp_%s%d" % (name, blk), align_bytes=64, offset=group_at[name, blk]
-                )
-            else:
-                grouped[name, blk] = sb.tile([P, P, PACK], BF16, name="grp_%s%d" % (name, blk), align_bytes=64)
-            engine_copy(
-                grouped[name, blk][:].rearrange("p (c i) t -> p c t i", i=4),
-                raw[name, blk].rearrange("p t (c i) -> p c t i", i=4),
-            )
-
-        def quantize(name, blk):
-            if (name, blk) in codes_at:
-                w_codes[name, blk] = lap.tile(
-                    [P, P], U32, name="wc_%s%d" % (name, blk), align_bytes=64, offset=codes_at[name, blk]
-                )
-            else:
-                w_codes[name, blk] = sb.tile([P, P], U32, name="wc_%s%d" % (name, blk), align_bytes=64)
-            w_plane[name, blk] = sb.tile([P, P], U8, name="wp_%s%d" % (name, blk), align_bytes=64)
-            nc.vector.quantize_mx(
-                out=w_codes[name, blk][:].bitcast(FP8X4),
-                scales=w_plane[name, blk][:],
-                in_=grouped[name, blk][:].rearrange("p c t -> p (c t)"),
-            )
-
-        banks = {}
-
-        def product(name, blk, c0, n, b):
-            banks[name, blk, c0] = (bank_tile(b), n)
-            half, at = divmod(c0, BANK)
-            nc.tensor.matmul_mx(
-                out=banks[name, blk, c0][0][:, 0:n],
-                lhsT=w_codes[name, blk][:].bitcast(FP8X4),
-                lhsT_scale=w_plane[name, blk][:],
-                rhs=x_codes[half][:, at : at + n].bitcast(FP8X4),
-                rhs_scale=x_plane[:, c0 : c0 + n],
-                start=True,
-                stop=True,
-            )
-
-        def empty(name, blk, c0):
-            if (name, blk) not in rows:
-                rows[name, blk] = sb.tile([P, S], F32, name="rows_%s%d" % (name, blk))
-            bank, n = banks[name, blk, c0]
-            nc.scalar.copy(rows[name, blk][:, c0 : c0 + n], bank[:, 0:n])
-
-        at_cen = {}
-        cen_at = {("g", 0): 6176, ("s", 0): 12288}
-
-        def centre(name, blk):
-            if (name, blk) in cen_at:
-                at_cen[name, blk] = lap.tile([P, V], F32, name="cen_%s%d" % (name, blk), offset=cen_at[name, blk])
-            else:
-                at_cen[name, blk] = sb.tile([P, V], F32, name="cen_%s%d" % (name, blk))
-            nc.vector.tensor_copy(at_cen[name, blk][:], rows[name, blk][:].indirect(lists["cen"][:]))
-
-        def scaled(blk, d, c0, c1):
-            u = sb.tile([P, c1 - c0], F32, name="u_%d_%d_%d" % (blk, d, c0))
-            offsets = lists["pos%d" % (d + 1)][:, c0 // LIST_GROUP : c1 // LIST_GROUP]
-            nc.vector.tensor_tensor(u[:], rows["h", blk][:].indirect(offsets), at_cen["g", blk][:, c0:c1], MULT)
-            return u
-
-        def turn(bank, src, n, start, stop):
-            for j in range(n // P):
-                nc.tensor.matmul(
-                    bank[:, j * P : (j + 1) * P],
-                    lhsT=src[:, j * P : (j + 1) * P],
-                    rhs=ident[:],
-                    is_transpose=True,
-                    start=start and j == 0,
-                    stop=stop and j == n // P - 1,
-                )
-
-        def relu_of(z, name, c0=0, c1=BANK):
-            if name in relu_at:
-                r = lap.tile([P, c1 - c0], F32, name=name, offset=relu_at[name])
-            else:
-                r = sb.tile([P, c1 - c0], F32, name=name)
-            nc.scalar.activation(r[:], z[:, c0:c1], RELU)
-            return r
-
-        vcopy, scopy = nc.vector.tensor_copy, nc.scalar.copy
-        H = V // 2
-
         cast("g", 0, scopy)
-        load_whole("h", w3, lap.tile([P, PACK, N], F32, name="raw_h", offset=6176))
-        load_half("g", w1, 1, lap.tile([P, PACK, P], F32, name="raw_g1", offset=12256))
+        load_whole("s", w2)
+        load_half("g", w1, 1)
         quantize("g", 0)
         pick_words(0)
         pick_words(1)
-        for blk in range(2):
-            cast("s", blk, scopy)
-        product("g", 0, 0, BANK, 0)
-        product("g", 0, BANK, H, 1)
-        product("g", 0, BANK + H, H, 2)
-        for blk in range(2):
-            quantize("s", blk)
-        for blk in range(2):
-            cast("h", blk, vcopy)
-        for blk in range(2):
-            quantize("h", blk)
-        for c0 in (0, BANK, BANK + H):
-            empty("g", 0, c0)
-        for name, bs in (("s", (0, 1)), ("h", (2, 0))):
-            for half in range(2):
-                product(name, 0, half * BANK, BANK, bs[half])
-                empty(name, 0, half * BANK)
+        cast("h", 0, scopy)
+        product("g", 0, 0, 0)
+        empty("g", 0, 0, scopy)
+        quantize("h", 0)
+        product("g", 0, BANK, 1, HALF)
+        product("g", 0, BANK + HALF, 6, HALF)
+        empty("g", 0, BANK, scopy)
+        empty("g", 0, BANK + HALF, scopy)
+        cast_whole("s", vcopy)
+        cast("g", 1, gcopy)
+        cast("h", 1, gcopy)
+        product("h", 0, 0, 2)
+        product("h", 0, BANK, 3)
+        quantize_whole("s")
         centre("g", 0)
-        cast("g", 1, vcopy)
-        centre("s", 0)
+        empty("h", 0, 0, vcopy)
+        empty("h", 0, BANK, vcopy)
         quantize("g", 1)
-        for half in range(2):
-            product("g", 1, half * BANK, BANK, 1 + half)
-            empty("g", 1, half * BANK)
-        product("s", 1, 0, BANK, 0)
-        empty("s", 1, 0)
-
-        shift = at_cen["s", 0]
-        z0 = bank_tile(3)
-        turn(z0, shift, V, True, False)
-        product("s", 1, BANK, BANK, 1)
-        u = scaled(0, 0, 0, V)
-        turn(z0, u, V, False, True)
-        product("h", 1, 0, BANK, 2)
-        r = relu_of(z0, "r00")
-        empty("s", 1, BANK)
-        empty("h", 1, 0)
-        z1 = bank_tile(4)
-        turn(z1, shift, V, True, False)
-        product("h", 1, BANK, BANK, 0)
-        u = scaled(0, 1, 0, V)
-        turn(z1, u, V, False, True)
-        acc0 = bank_tile(5)
-        turn(acc0, r, V, True, False)
-        r = relu_of(z1, "r01")
-        empty("h", 1, BANK)
-        z2 = bank_tile(1)
-        turn(z2, shift, V, True, False)
-        u = scaled(0, 2, 0, V)
-        turn(z2, u, V, False, True)
-        turn(acc0, r, V, False, False)
-        r = relu_of(z2, "r02")
-        turn(acc0, r, V, False, True)
+        product("s", 0, 0, 4)
+        product("s", 0, BANK, 5)
+        product("g", 1, 0, 0)
+        product("g", 1, BANK, 1)
+        u0 = [scaled(0, 0)]
+        quantize("h", 1)
+        u0 += [scaled(0, d) for d in (1, 2)]
+        empty("s", 0, 0, scopy)
+        empty("s", 0, BANK, scopy)
+        empty("g", 1, 0, scopy)
+        product("h", 1, 0, 0)
+        product("h", 1, BANK, 5)
+        empty("g", 1, BANK, scopy)
+        centre("s", 0)
+        z0 = [bank_tile(6), bank_tile(7)]
+        turn(z0[0], u0[0][:], True, False)
+        turn(z0[1], u0[1][:], True, False)
+        turn(z0[0], at_cen["s", 0][:], False, True)
+        turn(z0[1], at_cen["s", 0][:], False, True)
         centre("g", 1)
-        centre("s", 1)
-        res0 = sb.tile([P, V], F32, name="res0")
-        nc.scalar.copy(res0[:], acc0[:])
-        nc.scalar.dma_start(out=out[0:P, :], in_=res0[:])
+        z02 = shifted(u0[2][:], 0, 0, "z02", nc.gpsimd)
+        for half in range(2):
+            empty("h", 1, half * BANK, vcopy)
+            product("s", 1, half * BANK, (0, 5)[half])
+        acc0 = bank_tile(1)
+        r = relu_of(z0[0][:], "r00")
+        turn(acc0, r[:], True, False)
+        for half in range(2):
+            empty("s", 1, half * BANK, scopy)
+        r = relu_of(z0[1][:], "r01")
+        turn(acc0, r[:], False, True)
 
-        shift = at_cen["s", 1]
-        zs = {}
-        for (a, d), b in zip(((0, 0), (0, 1), (1, 0), (1, 1)), (1, 4, 3, 0)):
-            zs[a, d] = bank_tile(b)
-            turn(zs[a, d], shift[:, a * H : (a + 1) * H], H, True, False)
-        accs = [bank_tile(b) for b in (6, 7)]
+        u1 = [scaled(1, d) for d in range(2)]
+        z1 = {(d, a): bank_tile(b) for d, a, b in ((0, 0, 6), (0, 1, 4), (1, 0, 7), (1, 1, 5))}
+        for a in range(2):
+            turn(z1[0, a], u1[0][:, a * HALF : (a + 1) * HALF], True, False)
+        u12 = [scaled(1, 2, a * HALF, (a + 1) * HALF) for a in range(2)]
+        finish(z02[:], acc0[:], 0, 0, nc.sync)
+        for a in range(2):
+            centre("s", 1, a * HALF, (a + 1) * HALF)
+        for a in range(2):
+            turn(z1[1, a], u1[1][:, a * HALF : (a + 1) * HALF], True, False)
         for a in range(2):
             for d in range(2):
-                u = scaled(1, d, a * H, (a + 1) * H)
-                turn(zs[a, d], u, H, False, True)
+                turn(z1[d, a], at_cen["s", 1][:, a * HALF : (a + 1) * HALF], False, True)
+        acc1 = [bank_tile(2), bank_tile(3)]
+        for a in range(2):
             for d in range(2):
-                r = relu_of(zs[a, d], "r1%d_%d" % (d, a), 0, H)
-                turn(accs[a], r, H, d == 0, d == 1)
-        us = [scaled(1, 2, a * H, (a + 1) * H) for a in range(2)]
-        zt = []
+                r = relu_of(z1[d, a][:, 0:HALF], "r1%d_%d" % (d, a))
+                turn(acc1[a], r[:], d == 0, d == 1)
+        z12 = [shifted(u12[a][:], 1, a * HALF, "z12_%d" % a) for a in range(2)]
         for a in range(2):
-            z = sb.tile([P, H], F32, name="z_tail%d" % a)
-            nc.vector.tensor_tensor(z[:], us[a][:], shift[:, a * H : (a + 1) * H], ADD)
-            zt.append(z)
-        for a in range(2):
-            res = sb.tile([P, H], F32, name="res1_%d" % a)
-            nc.vector.scalar_tensor_tensor(res[:], zt[a][:], 0.0, accs[a][:, 0:H], MAX, ADD)
-            nc.sync.dma_start(out=out[P : 2 * P, a * H : (a + 1) * H], in_=res[:])
+            finish(z12[a][:], acc1[a][:, 0:HALF], 1, a * HALF, nc.sync)

@@ -37,7 +37,7 @@ def tile_picked_filmg_relu_p_kernel(
         ps = ctx.enter_context(tc.psum_pool(name="ps", bufs=1))
         vcopy, scopy = nc.vector.tensor_copy, nc.scalar.copy
         lists, raw, grouped, w_codes, w_plane, banks, rows, at_cen, x_codes = {}, {}, {}, {}, {}, {}, {}, {}, {}
-        place = {}
+        place, sent = {}, {}
 
         def tile(shape, dtype, name, **kw):
             if name in place:
@@ -139,9 +139,11 @@ def tile_picked_filmg_relu_p_kernel(
                 nc.scalar.activation(at_cen[name, blk][:, c0:c1], picked, COPY)
 
         def scaled(blk, d, c0=0, c1=V):
-            u = tile([P, c1 - c0], F32, "u_%d_%d_%d" % (blk, d, c0))
+            if blk not in sent:
+                sent[blk] = tile([P, 3 * V], F32, "u_%d" % blk)
+            u = sent[blk][:, d * V + c0 : d * V + c1]
             picked = rows["h", blk][:].indirect(offsets("pos%d" % (d + 1), c0, c1))
-            nc.vector.tensor_tensor(u[:], picked, at_cen["g", blk][:, c0:c1], MULT)
+            nc.vector.tensor_tensor(u, picked, at_cen["g", blk][:, c0:c1], MULT)
             return u
 
         def turn(bank, src, start, stop):
@@ -173,8 +175,8 @@ def tile_picked_filmg_relu_p_kernel(
             nc.vector.scalar_tensor_tensor(res[:], z, 0.0, acc, MAX, ADD)
             queue.dma_start(out=out[blk * P : (blk + 1) * P, c0 : c0 + n], in_=res[:])
 
-        place.update({"raw_g0": 3072, "raw_s": 0, "raw_g1": 4096, "grp_h1": 5056, "u_0_0_0": 6112})
-        place.update({"grp_s": 8192, "rows_h0": 8192, "wc_g1": 12288, "cen_s0": 12288})
+        place.update({"raw_g0": 3072, "raw_s": 0, "raw_g1": 4096, "grp_h1": 5056, "u_0": 6112})
+        place.update({"grp_s": 12288, "rows_h0": 12288, "wc_g1": 16384, "cen_s0": 16384, "wp_g1": 18432, "wp_h1": 18432})
         first = P - SCALE_ROWS
         scale_table = sb.tile([P, T], U8, name="scale_table")
         nc.sync.dma_start(out=scale_table[first:P, :].bitcast(I32), in_=x_scales[0].bitcast(I32))
@@ -226,8 +228,8 @@ def tile_picked_filmg_relu_p_kernel(
         empty("h", 0, 0, vcopy)
         empty("h", 0, BANK, vcopy)
         quantize("g", 1)
-        product("s", 0, 0, 4)
-        product("s", 0, BANK, 5)
+        product("s", 0, 0, 6)
+        product("s", 0, BANK, 2)
         product("g", 1, 0, 0)
         product("g", 1, BANK, 1)
         u0 = [scaled(0, 0)]
@@ -237,29 +239,29 @@ def tile_picked_filmg_relu_p_kernel(
         empty("s", 0, BANK, scopy)
         empty("g", 1, 0, scopy)
         product("h", 1, 0, 0)
-        product("h", 1, BANK, 5)
+        product("h", 1, BANK, 6)
         empty("g", 1, BANK, scopy)
         centre("s", 0)
-        z0 = [bank_tile(6), bank_tile(7)]
-        turn(z0[0], u0[0][:], True, False)
-        turn(z0[1], u0[1][:], True, False)
+        z0 = [bank_tile(4), bank_tile(5)]
+        turn(z0[0], u0[0], True, False)
+        turn(z0[1], u0[1], True, False)
         turn(z0[0], at_cen["s", 0][:], False, True)
         turn(z0[1], at_cen["s", 0][:], False, True)
         centre("g", 1)
-        z02 = shifted(u0[2][:], 0, 0, "z02", nc.gpsimd)
+        z02 = shifted(u0[2], 0, 0, "z02", nc.gpsimd)
         for half in range(2):
             empty("h", 1, half * BANK, vcopy)
-            product("s", 1, half * BANK, (0, 5)[half])
+            product("s", 1, half * BANK, (0, 6)[half])
         acc0 = bank_tile(1)
+        empty("s", 1, 0, scopy)
         r = relu_of(z0[0][:], "r00")
         turn(acc0, r[:], True, False)
-        for half in range(2):
-            empty("s", 1, half * BANK, scopy)
+        empty("s", 1, BANK, scopy)
         r = relu_of(z0[1][:], "r01")
         turn(acc0, r[:], False, True)
 
         u1 = [scaled(1, d) for d in range(2)]
-        z1 = {(d, a): bank_tile(b) for d, a, b in ((0, 0, 6), (0, 1, 4), (1, 0, 7), (1, 1, 5))}
+        z1 = {(d, a): bank_tile(b) for d, a, b in ((0, 0, 4), (0, 1, 2), (1, 0, 5), (1, 1, 6))}
         for a in range(2):
             turn(z1[0, a], u1[0][:, a * HALF : (a + 1) * HALF], True, False)
         u12 = [scaled(1, 2, a * HALF, (a + 1) * HALF) for a in range(2)]
@@ -271,11 +273,11 @@ def tile_picked_filmg_relu_p_kernel(
         for a in range(2):
             for d in range(2):
                 turn(z1[d, a], at_cen["s", 1][:, a * HALF : (a + 1) * HALF], False, True)
-        acc1 = [bank_tile(2), bank_tile(3)]
+        acc1 = [bank_tile(3), bank_tile(7)]
         for a in range(2):
             for d in range(2):
                 r = relu_of(z1[d, a][:, 0:HALF], "r1%d_%d" % (d, a))
                 turn(acc1[a], r[:], d == 0, d == 1)
-        z12 = [shifted(u12[a][:], 1, a * HALF, "z12_%d" % a) for a in range(2)]
+        z12 = [shifted(u12[a], 1, a * HALF, "z12_%d" % a) for a in range(2)]
         for a in range(2):
             finish(z12[a][:], acc1[a][:, 0:HALF], 1, a * HALF, nc.sync)

@@ -175,8 +175,8 @@ def tile_picked_filmg_relu_p_kernel(
             nc.vector.scalar_tensor_tensor(res[:], z, 0.0, acc, MAX, ADD)
             queue.dma_start(out=out[blk * P : (blk + 1) * P, c0 : c0 + n], in_=res[:])
 
-        place.update({"raw_g0": 3072, "raw_s": 0, "raw_g1": 4096, "grp_h1": 5056, "u_0": 6112})
-        place.update({"grp_s": 12288, "rows_h0": 12288, "wc_g1": 16384, "cen_s0": 16384, "wp_g1": 18432, "wp_h1": 18432})
+        place.update({"raw_g0": 3072, "raw_s": 0, "raw_g1": 4096, "u_0": 6112})
+        place.update({"grp_s": 12288, "rows_h0": 12288, "wc_g1": 16384, "cen_s0": 16384, "rows_s1": 16896})
         first = P - SCALE_ROWS
         scale_table = sb.tile([P, T], U8, name="scale_table")
         nc.sync.dma_start(out=scale_table[first:P, :].bitcast(I32), in_=x_scales[0].bitcast(I32))
@@ -211,6 +211,7 @@ def tile_picked_filmg_relu_p_kernel(
         pick_words(0)
         pick_words(1)
         cast("h", 0, scopy)
+        cast("h", 1, gcopy)
         product("g", 0, 0, 0)
         empty("g", 0, 0, scopy)
         quantize("h", 0)
@@ -220,7 +221,7 @@ def tile_picked_filmg_relu_p_kernel(
         empty("g", 0, BANK + HALF, scopy)
         cast_whole("s", vcopy)
         cast("g", 1, gcopy)
-        cast("h", 1, gcopy)
+        quantize("h", 1)
         product("h", 0, 0, 2)
         product("h", 0, BANK, 3)
         quantize_whole("s")
@@ -229,18 +230,18 @@ def tile_picked_filmg_relu_p_kernel(
         empty("h", 0, BANK, vcopy)
         quantize("g", 1)
         product("s", 0, 0, 6)
-        product("s", 0, BANK, 2)
+        product("s", 0, BANK, 7)
         product("g", 1, 0, 0)
         product("g", 1, BANK, 1)
-        u0 = [scaled(0, 0)]
-        quantize("h", 1)
-        u0 += [scaled(0, d) for d in (1, 2)]
+        u0 = [scaled(0, d) for d in range(3)]
         empty("s", 0, 0, scopy)
+        product("h", 1, 0, 6)
         empty("s", 0, BANK, scopy)
+        product("h", 1, BANK, 7)
         empty("g", 1, 0, scopy)
-        product("h", 1, 0, 0)
-        product("h", 1, BANK, 6)
+        product("s", 1, 0, 0)
         empty("g", 1, BANK, scopy)
+        product("s", 1, BANK, 1)
         centre("s", 0)
         z0 = [bank_tile(4), bank_tile(5)]
         turn(z0[0], u0[0], True, False)
@@ -251,17 +252,16 @@ def tile_picked_filmg_relu_p_kernel(
         z02 = shifted(u0[2], 0, 0, "z02", nc.gpsimd)
         for half in range(2):
             empty("h", 1, half * BANK, vcopy)
-            product("s", 1, half * BANK, (0, 6)[half])
-        acc0 = bank_tile(1)
-        empty("s", 1, 0, scopy)
+        acc0 = bank_tile(2)
         r = relu_of(z0[0][:], "r00")
         turn(acc0, r[:], True, False)
-        empty("s", 1, BANK, scopy)
         r = relu_of(z0[1][:], "r01")
         turn(acc0, r[:], False, True)
+        empty("s", 1, 0, scopy)
+        empty("s", 1, BANK, scopy)
 
         u1 = [scaled(1, d) for d in range(2)]
-        z1 = {(d, a): bank_tile(b) for d, a, b in ((0, 0, 4), (0, 1, 2), (1, 0, 5), (1, 1, 6))}
+        z1 = {(d, a): bank_tile(b) for d, a, b in ((0, 0, 4), (0, 1, 5), (1, 0, 0), (1, 1, 1))}
         for a in range(2):
             turn(z1[0, a], u1[0][:, a * HALF : (a + 1) * HALF], True, False)
         u12 = [scaled(1, 2, a * HALF, (a + 1) * HALF) for a in range(2)]
@@ -273,7 +273,7 @@ def tile_picked_filmg_relu_p_kernel(
         for a in range(2):
             for d in range(2):
                 turn(z1[d, a], at_cen["s", 1][:, a * HALF : (a + 1) * HALF], False, True)
-        acc1 = [bank_tile(3), bank_tile(7)]
+        acc1 = [bank_tile(3), bank_tile(6)]
         for a in range(2):
             for d in range(2):
                 r = relu_of(z1[d, a][:, 0:HALF], "r1%d_%d" % (d, a))

@@ -176,7 +176,8 @@ def tile_picked_filmg_relu_p_kernel(
             queue.dma_start(out=out[blk * P : (blk + 1) * P, c0 : c0 + n], in_=res[:])
 
         place.update({"raw_g0": 3072, "raw_s": 0, "raw_g1": 4096, "u_0": 6112})
-        place.update({"grp_s": 12288, "rows_h0": 12288, "wc_g1": 16384, "cen_s0": 16384, "rows_s1": 16896})
+        place.update({"grp_s0": 12288, "cen_g0": 12800, "wc_h1": 12288, "wc_g1": 16384, "cen_s0": 16384, "rows_s1": 16896})
+        place.update({"wp_g1": 21504, "rows_h1": 21504})
         first = P - SCALE_ROWS
         scale_table = sb.tile([P, T], U8, name="scale_table")
         nc.sync.dma_start(out=scale_table[first:P, :].bitcast(I32), in_=x_scales[0].bitcast(I32))
@@ -219,40 +220,42 @@ def tile_picked_filmg_relu_p_kernel(
         product("g", 0, BANK + HALF, 6, HALF)
         empty("g", 0, BANK, scopy)
         empty("g", 0, BANK + HALF, scopy)
-        cast_whole("s", vcopy)
+        cast("s", 0, vcopy)
+        cast("s", 1, vcopy)
         cast("g", 1, gcopy)
-        quantize("h", 1)
         product("h", 0, 0, 2)
         product("h", 0, BANK, 3)
-        quantize_whole("s")
-        centre("g", 0)
-        empty("h", 0, 0, vcopy)
-        empty("h", 0, BANK, vcopy)
+        quantize("s", 0)
+        quantize("s", 1)
+        quantize("h", 1)
+        centre("g", 0, on_vector=True)
+        empty("h", 0, 0, scopy)
+        empty("h", 0, BANK, scopy)
         quantize("g", 1)
         product("s", 0, 0, 6)
         product("s", 0, BANK, 7)
         product("g", 1, 0, 0)
         product("g", 1, BANK, 1)
+        product("h", 1, 0, 2)
+        product("h", 1, BANK, 3)
         u0 = [scaled(0, d) for d in range(3)]
         empty("s", 0, 0, scopy)
-        product("h", 1, 0, 6)
+        product("s", 1, 0, 6)
         empty("s", 0, BANK, scopy)
-        product("h", 1, BANK, 7)
+        product("s", 1, BANK, 7)
         empty("g", 1, 0, scopy)
-        product("s", 1, 0, 0)
         empty("g", 1, BANK, scopy)
-        product("s", 1, BANK, 1)
         centre("s", 0)
         z0 = [bank_tile(4), bank_tile(5)]
         turn(z0[0], u0[0], True, False)
         turn(z0[1], u0[1], True, False)
         turn(z0[0], at_cen["s", 0][:], False, True)
         turn(z0[1], at_cen["s", 0][:], False, True)
-        centre("g", 1)
+        centre("g", 1, on_vector=True)
         z02 = shifted(u0[2], 0, 0, "z02", nc.gpsimd)
         for half in range(2):
-            empty("h", 1, half * BANK, vcopy)
-        acc0 = bank_tile(2)
+            empty("h", 1, half * BANK, scopy)
+        acc0 = bank_tile(0)
         r = relu_of(z0[0][:], "r00")
         turn(acc0, r[:], True, False)
         r = relu_of(z0[1][:], "r01")
@@ -260,24 +263,24 @@ def tile_picked_filmg_relu_p_kernel(
         empty("s", 1, 0, scopy)
         empty("s", 1, BANK, scopy)
 
-        u1 = [scaled(1, d) for d in range(2)]
-        z1 = {(d, a): bank_tile(b) for d, a, b in ((0, 0, 4), (0, 1, 5), (1, 0, 0), (1, 1, 1))}
+        u1 = [scaled(1, d) for d in range(3)]
+        z1 = [bank_tile(4), bank_tile(5)]
         for a in range(2):
-            turn(z1[0, a], u1[0][:, a * HALF : (a + 1) * HALF], True, False)
-        u12 = [scaled(1, 2, a * HALF, (a + 1) * HALF) for a in range(2)]
+            turn(z1[a], u1[0][:, a * HALF : (a + 1) * HALF], True, False)
         finish(z02[:], acc0[:], 0, 0, nc.sync)
         for a in range(2):
             centre("s", 1, a * HALF, (a + 1) * HALF)
+            turn(z1[a], at_cen["s", 1][:, a * HALF : (a + 1) * HALF], False, True)
+        acc1 = [bank_tile(1), bank_tile(2)]
         for a in range(2):
-            turn(z1[1, a], u1[1][:, a * HALF : (a + 1) * HALF], True, False)
+            r = relu_of(z1[a][:, 0:HALF], "r10_%d" % a)
+            turn(acc1[a], r[:], True, True)
+        z11 = shifted(u1[1], 1, 0, "z11")
+        z12 = shifted(u1[2], 1, 0, "z12")
+        part = tile([P, V], F32, "part")
         for a in range(2):
-            for d in range(2):
-                turn(z1[d, a], at_cen["s", 1][:, a * HALF : (a + 1) * HALF], False, True)
-        acc1 = [bank_tile(3), bank_tile(6)]
+            cols = slice(a * HALF, (a + 1) * HALF)
+            nc.vector.scalar_tensor_tensor(part[:, cols], z11[:, cols], 0.0, acc1[a][:, 0:HALF], MAX, ADD)
         for a in range(2):
-            for d in range(2):
-                r = relu_of(z1[d, a][:, 0:HALF], "r1%d_%d" % (d, a))
-                turn(acc1[a], r[:], d == 0, d == 1)
-        z12 = [shifted(u12[a], 1, a * HALF, "z12_%d" % a) for a in range(2)]
-        for a in range(2):
-            finish(z12[a][:], acc1[a][:, 0:HALF], 1, a * HALF, nc.sync)
+            cols = slice(a * HALF, (a + 1) * HALF)
+            finish(z12[:, cols], part[:, cols], 1, a * HALF, nc.sync)

@@ -176,8 +176,8 @@ def tile_picked_filmg_relu_p_kernel(
             queue.dma_start(out=out[blk * P : (blk + 1) * P, c0 : c0 + n], in_=res[:])
 
         place.update({"raw_g0": 3072, "raw_s": 0, "raw_g1": 4096, "u_0": 6112})
-        place.update({"grp_s0": 12288, "cen_g0": 12800, "wc_h1": 12288, "wc_g1": 16384, "cen_s0": 16384, "rows_s1": 16896})
-        place.update({"wp_g1": 21504, "rows_h1": 21504})
+        place.update({"grp_s0": 12288, "cen_g0": 12800, "wc_h1": 12288, "wc_g1": 16384, "cen_s0": 16384})
+        place.update({"wp_g1": 21504, "rows_h1": 21504, "rows_s0": 25600, "rows_s1": 25600, "r01": 29696, "z12": 29696})
         first = P - SCALE_ROWS
         scale_table = sb.tile([P, T], U8, name="scale_table")
         nc.sync.dma_start(out=scale_table[first:P, :].bitcast(I32), in_=x_scales[0].bitcast(I32))
@@ -258,29 +258,33 @@ def tile_picked_filmg_relu_p_kernel(
         acc0 = bank_tile(0)
         r = relu_of(z0[0][:], "r00")
         turn(acc0, r[:], True, False)
-        r = relu_of(z0[1][:], "r01")
-        turn(acc0, r[:], False, True)
         empty("s", 1, 0, scopy)
         empty("s", 1, BANK, scopy)
+        r = relu_of(z0[1][:], "r01")
+        turn(acc0, r[:], False, True)
 
         u1 = [scaled(1, d) for d in range(3)]
-        z1 = [bank_tile(4), bank_tile(5)]
-        for a in range(2):
-            turn(z1[a], u1[0][:, a * HALF : (a + 1) * HALF], True, False)
+        lo, hi = slice(0, HALF), slice(HALF, V)
+        z10, z11 = [bank_tile(4), bank_tile(6)], bank_tile(5)
+        turn(z10[0], u1[0][:, lo], True, False)
+        turn(z10[1], u1[0][:, hi], True, False)
+        turn(z11, u1[1][:, hi], True, False)
         finish(z02[:], acc0[:], 0, 0, nc.sync)
-        for a in range(2):
-            centre("s", 1, a * HALF, (a + 1) * HALF)
-            turn(z1[a], at_cen["s", 1][:, a * HALF : (a + 1) * HALF], False, True)
+        centre("s", 1, 0, HALF)
+        turn(z10[0], at_cen["s", 1][:, lo], False, True)
+        centre("s", 1, HALF, V)
+        turn(z10[1], at_cen["s", 1][:, hi], False, True)
+        turn(z11, at_cen["s", 1][:, hi], False, True)
         acc1 = [bank_tile(1), bank_tile(2)]
-        for a in range(2):
-            r = relu_of(z1[a][:, 0:HALF], "r10_%d" % a)
-            turn(acc1[a], r[:], True, True)
-        z11 = shifted(u1[1], 1, 0, "z11")
+        r = relu_of(z10[0][:, lo], "r10_0")
+        turn(acc1[0], r[:], True, True)
+        r = relu_of(z10[1][:, lo], "r10_1")
+        turn(acc1[1], r[:], True, False)
+        r = relu_of(z11[:, lo], "r11_1")
+        turn(acc1[1], r[:], False, True)
+        z11_lo = shifted(u1[1][:, lo], 1, 0, "z11_lo", nc.gpsimd)
         z12 = shifted(u1[2], 1, 0, "z12")
-        part = tile([P, V], F32, "part")
-        for a in range(2):
-            cols = slice(a * HALF, (a + 1) * HALF)
-            nc.vector.scalar_tensor_tensor(part[:, cols], z11[:, cols], 0.0, acc1[a][:, 0:HALF], MAX, ADD)
-        for a in range(2):
-            cols = slice(a * HALF, (a + 1) * HALF)
-            finish(z12[:, cols], part[:, cols], 1, a * HALF, nc.sync)
+        part = tile([P, HALF], F32, "part")
+        nc.vector.scalar_tensor_tensor(part[:], z11_lo[:], 0.0, acc1[0][:, lo], MAX, ADD)
+        finish(z12[:, lo], part[:], 1, 0, nc.sync)
+        finish(z12[:, hi], acc1[1][:, lo], 1, HALF, nc.sync)

@@ -178,6 +178,7 @@ def tile_picked_filmg_relu_p_kernel(
         place.update({"raw_g0": 3072, "raw_s": 0, "raw_g1": 4096, "u_0": 6112})
         place.update({"grp_s0": 12288, "cen_g0": 12800, "wc_h1": 12288, "wc_g1": 16384, "cen_s0": 16384})
         place.update({"wp_g1": 21504, "rows_h1": 21504, "rows_s0": 25600, "rows_s1": 25600, "r01": 29696, "z12": 29696})
+        place.update({"grp_h1": 31744, "grp_g1": 31744})
         first = P - SCALE_ROWS
         scale_table = sb.tile([P, T], U8, name="scale_table")
         nc.sync.dma_start(out=scale_table[first:P, :].bitcast(I32), in_=x_scales[0].bitcast(I32))

@@ -178,7 +178,7 @@ def tile_picked_filmg_relu_p_kernel(
         place.update({"raw_g0": 3072, "raw_s": 0, "raw_g1": 4096, "u_0": 6112})
         place.update({"grp_s0": 12288, "cen_g0": 12800, "wc_h1": 12288, "wc_g1": 16384, "cen_s0": 16384})
         place.update({"wp_g1": 21504, "rows_h1": 21504, "rows_s0": 25600, "rows_s1": 25600, "r01": 29696, "z12": 29696})
-        place.update({"grp_h1": 31744, "grp_g1": 31744})
+        place.update({"grp_h1": 31744, "grp_g1": 31744, "r11_1": 32768, "res_1_0": 32768})
         first = P - SCALE_ROWS
         scale_table = sb.tile([P, T], U8, name="scale_table")
         nc.sync.dma_start(out=scale_table[first:P, :].bitcast(I32), in_=x_scales[0].bitcast(I32))
@@ -254,22 +254,25 @@ def tile_picked_filmg_relu_p_kernel(
         turn(z0[1], at_cen["s", 0][:], False, True)
         centre("g", 1, on_vector=True)
         z02 = shifted(u0[2], 0, 0, "z02", nc.gpsimd)
+        empty("s", 1, 0, vcopy)
         for half in range(2):
             empty("h", 1, half * BANK, scopy)
         acc0 = bank_tile(0)
         r = relu_of(z0[0][:], "r00")
         turn(acc0, r[:], True, False)
-        empty("s", 1, 0, scopy)
-        empty("s", 1, BANK, scopy)
         r = relu_of(z0[1][:], "r01")
         turn(acc0, r[:], False, True)
+        empty("s", 1, BANK, scopy)
 
-        u1 = [scaled(1, d) for d in range(3)]
         lo, hi = slice(0, HALF), slice(HALF, V)
+        u10 = scaled(1, 0)
+        u11_hi = scaled(1, 1, HALF, V)
+        u11_lo = scaled(1, 1, 0, HALF)
+        u12 = scaled(1, 2)
         z10, z11 = [bank_tile(4), bank_tile(6)], bank_tile(5)
-        turn(z10[0], u1[0][:, lo], True, False)
-        turn(z10[1], u1[0][:, hi], True, False)
-        turn(z11, u1[1][:, hi], True, False)
+        turn(z10[0], u10[:, lo], True, False)
+        turn(z10[1], u10[:, hi], True, False)
+        turn(z11, u11_hi, True, False)
         finish(z02[:], acc0[:], 0, 0, nc.sync)
         centre("s", 1, 0, HALF)
         turn(z10[0], at_cen["s", 1][:, lo], False, True)
@@ -283,9 +286,9 @@ def tile_picked_filmg_relu_p_kernel(
         turn(acc1[1], r[:], True, False)
         r = relu_of(z11[:, lo], "r11_1")
         turn(acc1[1], r[:], False, True)
-        z11_lo = shifted(u1[1][:, lo], 1, 0, "z11_lo", nc.gpsimd)
-        z12 = shifted(u1[2], 1, 0, "z12")
+        z11_lo = shifted(u11_lo, 1, 0, "z11_lo", nc.gpsimd)
+        z12 = shifted(u12, 1, 0, "z12")
         part = tile([P, HALF], F32, "part")
         nc.vector.scalar_tensor_tensor(part[:], z11_lo[:], 0.0, acc1[0][:, lo], MAX, ADD)
-        finish(z12[:, lo], part[:], 1, 0, nc.sync)
         finish(z12[:, hi], acc1[1][:, lo], 1, HALF, nc.sync)
+        finish(z12[:, lo], part[:], 1, 0, nc.sync)

@@ -78,6 +78,10 @@ def tile_picked_filmg_relu_p_kernel(
                 raw[name, blk].rearrange("p t (c i) -> p c t i", i=4),
             )
 
+        def cast_on_gpsimd(name, blk):
+            grouped[name, blk] = tile([P, P, PACK], BF16, "grp_%s%d" % (name, blk), align_bytes=64)
+            gcopy(grouped[name, blk][:], raw[name, blk].rearrange("p t c -> p c t"))
+
         def quantize(name, blk):
             w_codes[name, blk] = tile([P, P], U32, "wc_%s%d" % (name, blk), align_bytes=64)[:]
             w_plane[name, blk] = tile([P, P], U8, "wp_%s%d" % (name, blk), align_bytes=64)[:]
@@ -213,7 +217,7 @@ def tile_picked_filmg_relu_p_kernel(
         pick_words(0)
         pick_words(1)
         cast("h", 0, scopy)
-        cast("h", 1, gcopy)
+        cast_on_gpsimd("h", 1)
         product("g", 0, 0, 0)
         empty("g", 0, 0, scopy)
         quantize("h", 0)
@@ -223,13 +227,14 @@ def tile_picked_filmg_relu_p_kernel(
         empty("g", 0, BANK + HALF, scopy)
         cast("s", 0, vcopy)
         cast("s", 1, vcopy)
-        cast("g", 1, gcopy)
+        cast_on_gpsimd("g", 1)
         product("h", 0, 0, 2)
         product("h", 0, BANK, 3)
         quantize("s", 0)
         quantize("s", 1)
         quantize("h", 1)
-        centre("g", 0, on_vector=True)
+        centre("g", 0, 0, HALF, on_vector=True)
+        centre("g", 0, HALF, V, on_vector=True)
         empty("h", 0, 0, scopy)
         empty("h", 0, BANK, scopy)
         quantize("g", 1)
@@ -239,7 +244,9 @@ def tile_picked_filmg_relu_p_kernel(
         product("g", 1, BANK, 1)
         product("h", 1, 0, 2)
         product("h", 1, BANK, 3)
-        u0 = [scaled(0, d) for d in range(3)]
+        scaled(0, 0, 0, HALF)
+        scaled(0, 0, HALF, V)
+        u0 = [sent[0][:, 0:V], scaled(0, 1), scaled(0, 2)]
         empty("s", 0, 0, scopy)
         product("s", 1, 0, 6)
         empty("s", 0, BANK, scopy)

@@ -91,27 +91,12 @@ def tile_picked_filmg_relu_p_kernel(
                 in_=grouped[name, blk][:].rearrange("p c t -> p (c t)"),
             )
 
-        def cast_whole(name, engine_copy):
-            grouped[name] = tile([P, N, PACK], BF16, "grp_" + name, align_bytes=64)
-            engine_copy(
-                grouped[name][:].rearrange("p (c i) t -> p c t i", i=4),
-                raw[name].rearrange("p t (c i) -> p c t i", i=4),
-            )
-
-        def quantize_whole(name):
-            codes = tile([P, N], U32, "wc_" + name, align_bytes=64)
-            plane = tile([P, N], U8, "wp_" + name, align_bytes=64)
-            nc.vector.quantize_mx(
-                out=codes[:].bitcast(FP8X4), scales=plane[:], in_=grouped[name][:].rearrange("p c t -> p (c t)")
-            )
-            for blk in range(2):
-                w_codes[name, blk] = codes[:, blk * P : (blk + 1) * P]
-                w_plane[name, blk] = plane[:, blk * P : (blk + 1) * P]
-
-        def pick_words(half):
-            x_codes[half] = tile([P, BANK], U32, "x_codes%d" % half, align_bytes=64)
+        def pick_words(c0, c1):
+            half, at = divmod(c0, BANK)
+            if half not in x_codes:
+                x_codes[half] = tile([P, BANK], U32, "x_codes%d" % half, align_bytes=64)
             nc.vector.tensor_copy(
-                x_codes[half][:], word_table[:].bitcast(U32).indirect(offsets("offs", half * BANK, (half + 1) * BANK))
+                x_codes[half][:, at : at + c1 - c0], word_table[:].bitcast(U32).indirect(offsets("offs", c0, c1))
             )
 
         def product(name, blk, c0, b, n=BANK):
@@ -143,9 +128,7 @@ def tile_picked_filmg_relu_p_kernel(
                 nc.scalar.activation(at_cen[name, blk][:, c0:c1], picked, COPY)
 
         def scaled(blk, d, c0=0, c1=V):
-            if blk not in sent:
-                sent[blk] = tile([P, 3 * V], F32, "u_%d" % blk)
-            u = sent[blk][:, d * V + c0 : d * V + c1]
+            u = tile([P, c1 - c0], F32, "u_%d%d_%d" % (blk, d, c0))[:]
             picked = rows["h", blk][:].indirect(offsets("pos%d" % (d + 1), c0, c1))
             nc.vector.tensor_tensor(u, picked, at_cen["g", blk][:, c0:c1], MULT)
             return u
@@ -179,10 +162,11 @@ def tile_picked_filmg_relu_p_kernel(
             nc.vector.scalar_tensor_tensor(res[:], z, 0.0, acc, MAX, ADD)
             queue.dma_start(out=out[blk * P : (blk + 1) * P, c0 : c0 + n], in_=res[:])
 
-        place.update({"raw_g0": 3072, "raw_s": 0, "raw_g1": 4096, "u_0": 6112})
-        place.update({"grp_s0": 12288, "cen_g0": 12800, "wc_h1": 12288, "wc_g1": 16384, "cen_s0": 16384})
-        place.update({"wp_g1": 21504, "rows_h1": 21504, "rows_s0": 25600, "rows_s1": 25600, "r01": 29696, "z12": 29696})
-        place.update({"grp_h1": 31744, "grp_g1": 31744, "r11_1": 32768, "res_1_0": 32768})
+        place.update({"raw_g1": 0, "raw_g0": 1536, "raw_s": 3072})
+        place.update({"grp_g1": 8192, "grp_s0": 8192})
+        place.update({"wc_s0": 10240, "grp_s1": 10240})
+        place.update({"wp_h1": 12288, "wc_s1": 12288, "wc_h1": 14336, "u_01_0": 14336})
+        place.update({"u_02_0": 14336, "u_02_256": 15360, "z12_1": 14336})
         first = P - SCALE_ROWS
         scale_table = sb.tile([P, T], U8, name="scale_table")
         nc.sync.dma_start(out=scale_table[first:P, :].bitcast(I32), in_=x_scales[0].bitcast(I32))
@@ -211,91 +195,85 @@ def tile_picked_filmg_relu_p_kernel(
                 in_=picked_scales[first + 4 * q : first + 4 * q + 4, :].bitcast(I32),
             )
         cast("g", 0, scopy)
-        load_whole("s", w2)
         load_half("g", w1, 1)
+        load_whole("s", w2)
         quantize("g", 0)
-        pick_words(0)
-        pick_words(1)
+        pick_words(0, BANK)
+        pick_words(BANK, BANK + HALF)
+        pick_words(BANK + HALF, S)
         cast("h", 0, scopy)
         cast_on_gpsimd("h", 1)
         product("g", 0, 0, 0)
-        empty("g", 0, 0, scopy)
-        quantize("h", 0)
         product("g", 0, BANK, 1, HALF)
-        product("g", 0, BANK + HALF, 6, HALF)
+        product("g", 0, BANK + HALF, 2, HALF)
+        empty("g", 0, 0, scopy)
         empty("g", 0, BANK, scopy)
         empty("g", 0, BANK + HALF, scopy)
-        cast("s", 0, vcopy)
-        cast("s", 1, vcopy)
-        cast_on_gpsimd("g", 1)
-        product("h", 0, 0, 2)
-        product("h", 0, BANK, 3)
-        quantize("s", 0)
-        quantize("s", 1)
+        quantize("h", 0)
+        cast("g", 1, vcopy)
         quantize("h", 1)
-        centre("g", 0, 0, HALF, on_vector=True)
-        centre("g", 0, HALF, V, on_vector=True)
+        quantize("g", 1)
+        cast_on_gpsimd("s", 0)
+        product("h", 0, 0, 3)
+        product("h", 0, BANK, 4)
+        product("g", 1, 0, 5)
+        product("g", 1, BANK, 6)
+        centre("g", 0, on_vector=True)
         empty("h", 0, 0, scopy)
         empty("h", 0, BANK, scopy)
-        quantize("g", 1)
-        product("s", 0, 0, 6)
-        product("s", 0, BANK, 7)
-        product("g", 1, 0, 0)
-        product("g", 1, BANK, 1)
-        product("h", 1, 0, 2)
-        product("h", 1, BANK, 3)
-        scaled(0, 0, 0, HALF)
-        scaled(0, 0, HALF, V)
-        u0 = [sent[0][:, 0:V], scaled(0, 1), scaled(0, 2)]
-        empty("s", 0, 0, scopy)
-        product("s", 1, 0, 6)
-        empty("s", 0, BANK, scopy)
-        product("s", 1, BANK, 7)
+        quantize("s", 0)
+        product("s", 0, 0, 3)
+        product("s", 0, BANK, 4)
+        cast_on_gpsimd("s", 1)
+        u00 = scaled(0, 0)
         empty("g", 1, 0, scopy)
+        product("h", 1, 0, 5)
         empty("g", 1, BANK, scopy)
+        product("h", 1, BANK, 6)
+        z0 = [bank_tile(0), bank_tile(6)]
+        turn(z0[0], u00, True, False)
+        centre("g", 1, on_vector=True)
+        quantize("s", 1)
+        u01 = scaled(0, 1)
+        empty("s", 0, 0, scopy)
+        empty("s", 0, BANK, scopy)
+        product("s", 1, 0, 4)
+        empty("h", 1, 0, scopy)
+        product("s", 1, BANK, 5)
+        empty("h", 1, BANK, scopy)
+        turn(z0[1], u01, True, False)
+        u1 = [scaled(1, d) for d in range(3)]
         centre("s", 0)
-        z0 = [bank_tile(4), bank_tile(5)]
-        turn(z0[0], u0[0], True, False)
-        turn(z0[1], u0[1], True, False)
         turn(z0[0], at_cen["s", 0][:], False, True)
         turn(z0[1], at_cen["s", 0][:], False, True)
-        centre("g", 1, on_vector=True)
-        z02 = shifted(u0[2], 0, 0, "z02", nc.gpsimd)
-        empty("s", 1, 0, vcopy)
-        for half in range(2):
-            empty("h", 1, half * BANK, scopy)
-        acc0 = bank_tile(0)
+        empty("s", 1, 0, scopy)
+        empty("s", 1, BANK, scopy)
+        acc0 = bank_tile(2)
         r = relu_of(z0[0][:], "r00")
         turn(acc0, r[:], True, False)
+        halves = [slice(0, HALF), slice(HALF, V)]
+        z1 = {(0, 0): bank_tile(4), (1, 0): bank_tile(3), (0, 1): bank_tile(5), (1, 1): bank_tile(7)}
+        for d in range(2):
+            for i in range(2):
+                turn(z1[d, i], u1[d][:, halves[i]], True, False)
+        u02 = [scaled(0, 2, i * HALF, (i + 1) * HALF) for i in range(2)]
+        for i in range(2):
+            centre("s", 1, i * HALF, (i + 1) * HALF)
         r = relu_of(z0[1][:], "r01")
+        for d in range(2):
+            turn(z1[d, 0], at_cen["s", 1][:, halves[0]], False, True)
         turn(acc0, r[:], False, True)
-        empty("s", 1, BANK, scopy)
-
-        lo, hi = slice(0, HALF), slice(HALF, V)
-        u10 = scaled(1, 0)
-        u11_hi = scaled(1, 1, HALF, V)
-        u11_lo = scaled(1, 1, 0, HALF)
-        u12 = scaled(1, 2)
-        z10, z11 = [bank_tile(4), bank_tile(6)], bank_tile(5)
-        turn(z10[0], u10[:, lo], True, False)
-        turn(z10[1], u10[:, hi], True, False)
-        turn(z11, u11_hi, True, False)
-        finish(z02[:], acc0[:], 0, 0, nc.sync)
-        centre("s", 1, 0, HALF)
-        turn(z10[0], at_cen["s", 1][:, lo], False, True)
-        centre("s", 1, HALF, V)
-        turn(z10[1], at_cen["s", 1][:, hi], False, True)
-        turn(z11, at_cen["s", 1][:, hi], False, True)
-        acc1 = [bank_tile(1), bank_tile(2)]
-        r = relu_of(z10[0][:, lo], "r10_0")
-        turn(acc1[0], r[:], True, True)
-        r = relu_of(z10[1][:, lo], "r10_1")
-        turn(acc1[1], r[:], True, False)
-        r = relu_of(z11[:, lo], "r11_1")
-        turn(acc1[1], r[:], False, True)
-        z11_lo = shifted(u11_lo, 1, 0, "z11_lo", nc.gpsimd)
-        z12 = shifted(u12, 1, 0, "z12")
-        part = tile([P, HALF], F32, "part")
-        nc.vector.scalar_tensor_tensor(part[:], z11_lo[:], 0.0, acc1[0][:, lo], MAX, ADD)
-        finish(z12[:, hi], acc1[1][:, lo], 1, HALF, nc.sync)
-        finish(z12[:, lo], part[:], 1, 0, nc.sync)
+        for d in range(2):
+            turn(z1[d, 1], at_cen["s", 1][:, halves[1]], False, True)
+        acc1 = [bank_tile(0), bank_tile(6)]
+        for i in range(2):
+            for d in range(2):
+                r = relu_of(z1[d, i][:, 0:HALF], "r1%d_%d" % (d, i))
+                turn(acc1[i], r[:], d == 0, d == 1)
+        z12_lo = shifted(u1[2][:, halves[0]], 1, 0, "z12_0")
+        z02 = [shifted(u02[i], 0, i * HALF, "z02_%d" % i) for i in range(2)]
+        for i in range(2):
+            finish(z02[i][:], acc0[:, halves[i]], 0, i * HALF, nc.sync)
+        z12_hi = shifted(u1[2][:, halves[1]], 1, HALF, "z12_1", nc.gpsimd)
+        finish(z12_lo[:], acc1[0][:, 0:HALF], 1, 0, nc.sync)
+        finish(z12_hi[:], acc1[1][:, 0:HALF], 1, HALF, nc.sync)

@@ -162,11 +162,12 @@ def tile_picked_filmg_relu_p_kernel(
             nc.vector.scalar_tensor_tensor(res[:], z, 0.0, acc, MAX, ADD)
             queue.dma_start(out=out[blk * P : (blk + 1) * P, c0 : c0 + n], in_=res[:])
 
-        place.update({"raw_g1": 0, "raw_g0": 1536, "raw_s": 3072})
+        place.update({"raw_g1": 0, "ident_raw": 1792, "raw_s": 2048})
         place.update({"grp_g1": 8192, "grp_s0": 8192})
         place.update({"wc_s0": 10240, "grp_s1": 10240})
         place.update({"wp_h1": 12288, "wc_s1": 12288, "wc_h1": 14336, "u_01_0": 14336})
         place.update({"u_02_0": 14336, "u_02_256": 15360, "z12_1": 14336})
+        place.update({"raw_h": 18432, "rows_g0": 18432})
         first = P - SCALE_ROWS
         scale_table = sb.tile([P, T], U8, name="scale_table")
         nc.sync.dma_start(out=scale_table[first:P, :].bitcast(I32), in_=x_scales[0].bitcast(I32))
@@ -177,10 +178,9 @@ def tile_picked_filmg_relu_p_kernel(
         word_table = sb.tile([P, T], I32, name="word_table", align_bytes=64)
         nc.sync.dma_start(out=word_table[:], in_=x_words[0].rearrange("p n t -> p (n t)").bitcast(I32))
         load_whole("h", w3)
-        load_list("pos3", pos3)
 
         nc.vector.memset(scale_table[0:first, :].bitcast(I32), 0)
-        ident_raw = sb.tile([P, P], F32, name="ident_raw")
+        ident_raw = tile([P, P], F32, "ident_raw")
         make_identity(nc, ident_raw[:])
         ident = sb.tile([P, P], F32, name="ident")
         nc.scalar.activation(ident[:], ident_raw[:], RELU)
@@ -190,14 +190,15 @@ def tile_picked_filmg_relu_p_kernel(
         picked_scales = sb.tile([P, S], U8, name="picked_scales", align_bytes=64)
         nc.vector.tensor_copy(picked_scales[:], scale_table[:].indirect(lists["offs"][:]))
         for q in range(4):
-            nc.sync.dma_start(
+            nc.scalar.dma_start(
                 out=x_plane[32 * q : 32 * q + 4, :].bitcast(I32),
                 in_=picked_scales[first + 4 * q : first + 4 * q + 4, :].bitcast(I32),
             )
         cast("g", 0, scopy)
+        quantize("g", 0)
         load_half("g", w1, 1)
         load_whole("s", w2)
-        quantize("g", 0)
+        load_list("pos3", pos3)
         pick_words(0, BANK)
         pick_words(BANK, BANK + HALF)
         pick_words(BANK + HALF, S)

@@ -206,10 +206,12 @@ def tile_picked_filmg_relu_p_kernel(
         cast_on_gpsimd("h", 1)
         product("g", 0, 0, 0)
         product("g", 0, BANK, 1, HALF)
-        product("g", 0, BANK + HALF, 2, HALF)
+        product("g", 0, BANK + HALF, 2, P)
+        product("g", 0, S - P, 7, P)
         empty("g", 0, 0, scopy)
         empty("g", 0, BANK, scopy)
         empty("g", 0, BANK + HALF, scopy)
+        empty("g", 0, S - P, scopy)
         quantize("h", 0)
         cast("g", 1, vcopy)
         quantize("h", 1)
@@ -231,12 +233,12 @@ def tile_picked_filmg_relu_p_kernel(
         product("h", 1, 0, 5)
         empty("g", 1, BANK, scopy)
         product("h", 1, BANK, 6)
-        z0 = [bank_tile(0), bank_tile(6)]
-        turn(z0[0], u00, True, False)
+        z0 = [bank_tile(3), bank_tile(6)]
         centre("g", 1, on_vector=True)
         quantize("s", 1)
         u01 = scaled(0, 1)
         empty("s", 0, 0, scopy)
+        turn(z0[0], u00, True, False)
         empty("s", 0, BANK, scopy)
         product("s", 1, 0, 4)
         empty("h", 1, 0, scopy)
@@ -253,7 +255,7 @@ def tile_picked_filmg_relu_p_kernel(
         r = relu_of(z0[0][:], "r00")
         turn(acc0, r[:], True, False)
         halves = [slice(0, HALF), slice(HALF, V)]
-        z1 = {(0, 0): bank_tile(4), (1, 0): bank_tile(3), (0, 1): bank_tile(5), (1, 1): bank_tile(7)}
+        z1 = {(0, 0): bank_tile(4), (1, 0): bank_tile(0), (0, 1): bank_tile(5), (1, 1): bank_tile(7)}
         for d in range(2):
             for i in range(2):
                 turn(z1[d, i], u1[d][:, halves[i]], True, False)
@@ -266,7 +268,7 @@ def tile_picked_filmg_relu_p_kernel(
         turn(acc0, r[:], False, True)
         for d in range(2):
             turn(z1[d, 1], at_cen["s", 1][:, halves[1]], False, True)
-        acc1 = [bank_tile(0), bank_tile(6)]
+        acc1 = [bank_tile(3), bank_tile(6)]
         for i in range(2):
             for d in range(2):
                 r = relu_of(z1[d, i][:, 0:HALF], "r1%d_%d" % (d, i))

@@ -162,11 +162,10 @@ def tile_picked_filmg_relu_p_kernel(
             nc.vector.scalar_tensor_tensor(res[:], z, 0.0, acc, MAX, ADD)
             queue.dma_start(out=out[blk * P : (blk + 1) * P, c0 : c0 + n], in_=res[:])
 
-        place.update({"raw_g1": 0, "ident_raw": 1792, "raw_s": 2048})
-        place.update({"grp_g1": 8192, "grp_s0": 8192})
+        place.update({"raw_g1": 0, "ident_raw": 1792, "raw_s0": 2048, "picked_scales": 4096, "raw_s1": 4096})
         place.update({"wc_s0": 10240, "grp_s1": 10240})
         place.update({"wp_h1": 12288, "wc_s1": 12288, "wc_h1": 14336, "u_01_0": 14336})
-        place.update({"u_02_0": 14336, "u_02_256": 15360, "z12_1": 14336})
+        place.update({"u_02_0": 14336, "u_02_256": 15360, "z12_1": 15360})
         place.update({"raw_h": 18432, "rows_g0": 18432})
         first = P - SCALE_ROWS
         scale_table = sb.tile([P, T], U8, name="scale_table")
@@ -187,7 +186,7 @@ def tile_picked_filmg_relu_p_kernel(
         x_plane = sb.tile([P, S], U8, name="x_plane", align_bytes=64)
         nc.vector.memset(x_plane[:].bitcast(I32), 0)
 
-        picked_scales = sb.tile([P, S], U8, name="picked_scales", align_bytes=64)
+        picked_scales = tile([P, S], U8, "picked_scales", align_bytes=64)
         nc.vector.tensor_copy(picked_scales[:], scale_table[:].indirect(lists["offs"][:]))
         for q in range(4):
             nc.scalar.dma_start(
@@ -197,7 +196,8 @@ def tile_picked_filmg_relu_p_kernel(
         cast("g", 0, scopy)
         quantize("g", 0)
         load_half("g", w1, 1)
-        load_whole("s", w2)
+        load_half("s", w2, 0)
+        load_half("s", w2, 1)
         load_list("pos3", pos3)
         pick_words(0, BANK)
         pick_words(BANK, BANK + HALF)
@@ -216,33 +216,35 @@ def tile_picked_filmg_relu_p_kernel(
         cast("g", 1, vcopy)
         quantize("h", 1)
         quantize("g", 1)
-        cast_on_gpsimd("s", 0)
-        product("h", 0, 0, 3)
-        product("h", 0, BANK, 4)
-        product("g", 1, 0, 5)
-        product("g", 1, BANK, 6)
-        centre("g", 0, on_vector=True)
-        empty("h", 0, 0, scopy)
-        empty("h", 0, BANK, scopy)
+        cast("s", 0, vcopy)
         quantize("s", 0)
-        product("s", 0, 0, 3)
-        product("s", 0, BANK, 4)
+        for i in range(4):
+            product("h", 0, i * HALF, 3 + i, HALF)
+        product("g", 1, 0, 0)
+        product("g", 1, BANK, 1)
+        for c0 in (0, HALF):
+            centre("g", 0, c0, c0 + HALF, on_vector=True)
+        for i in range(4):
+            empty("h", 0, i * HALF, scopy)
+        product("s", 0, 0, 4)
+        product("s", 0, BANK, 6)
         cast_on_gpsimd("s", 1)
-        u00 = scaled(0, 0)
+        u00 = [scaled(0, 0, c0, c0 + HALF) for c0 in (0, HALF)]
         empty("g", 1, 0, scopy)
-        product("h", 1, 0, 5)
+        product("h", 1, 0, 0)
         empty("g", 1, BANK, scopy)
-        product("h", 1, BANK, 6)
-        z0 = [bank_tile(3), bank_tile(6)]
+        product("h", 1, BANK, 1)
+        z0 = [bank_tile(4), bank_tile(1)]
         centre("g", 1, on_vector=True)
         quantize("s", 1)
         u01 = scaled(0, 1)
         empty("s", 0, 0, scopy)
-        turn(z0[0], u00, True, False)
+        for i in range(2):
+            turn(z0[0][:, i * HALF : (i + 1) * HALF], u00[i], i == 0, False)
         empty("s", 0, BANK, scopy)
-        product("s", 1, 0, 4)
+        product("s", 1, 0, 6)
         empty("h", 1, 0, scopy)
-        product("s", 1, BANK, 5)
+        product("s", 1, BANK, 0)
         empty("h", 1, BANK, scopy)
         turn(z0[1], u01, True, False)
         u1 = [scaled(1, d) for d in range(3)]
@@ -255,7 +257,7 @@ def tile_picked_filmg_relu_p_kernel(
         r = relu_of(z0[0][:], "r00")
         turn(acc0, r[:], True, False)
         halves = [slice(0, HALF), slice(HALF, V)]
-        z1 = {(0, 0): bank_tile(4), (1, 0): bank_tile(0), (0, 1): bank_tile(5), (1, 1): bank_tile(7)}
+        z1 = {(0, 0): bank_tile(6), (1, 0): bank_tile(3), (0, 1): bank_tile(0), (1, 1): bank_tile(7)}
         for d in range(2):
             for i in range(2):
                 turn(z1[d, i], u1[d][:, halves[i]], True, False)
@@ -268,7 +270,7 @@ def tile_picked_filmg_relu_p_kernel(
         turn(acc0, r[:], False, True)
         for d in range(2):
             turn(z1[d, 1], at_cen["s", 1][:, halves[1]], False, True)
-        acc1 = [bank_tile(3), bank_tile(6)]
+        acc1 = [bank_tile(4), bank_tile(1)]
         for i in range(2):
             for d in range(2):
                 r = relu_of(z1[d, i][:, 0:HALF], "r1%d_%d" % (d, i))

from contextlib import ExitStack

import concourse.mybir as mybir
from concourse.masks import make_identity

K, T, S, V, N = 512, 4096, 1024, 512, 256
FLOPS = 3 * 2 * K * N * S

F32 = mybir.dt.float32
BF16 = mybir.dt.bfloat16
I32 = mybir.dt.int32
U32 = mybir.dt.uint32
U16 = mybir.dt.uint16
U8 = mybir.dt.uint8
FP8X4 = mybir.dt.float8_e4m3fn_x4
RELU = mybir.ActivationFunctionType.Relu
COPY = mybir.ActivationFunctionType.Copy
MULT = mybir.AluOpType.mult
ADD = mybir.AluOpType.add
MAX = mybir.AluOpType.max

P = 128
PACK = 4
BANK = 512
SCALE_ROWS = 16
LIST_GROUP = 16
HALF = V // 2


def tile_picked_filmg_relu_p_kernel(
    tc, x_words, x_scales, w1, w2, w3, offs, cen, pos1, pos2, pos3, out
):
    nc = tc.nc
    with ExitStack() as ctx:
        sb = ctx.enter_context(tc.tile_pool(name="sb", bufs=1))
        lap = ctx.enter_context(tc.tile_pool(name="lap", bufs=1))
        ps = ctx.enter_context(tc.psum_pool(name="ps", bufs=1))
        vcopy, scopy = nc.vector.tensor_copy, nc.scalar.copy
        lists, raw, grouped, w_codes, w_plane, banks, rows, at_cen, x_codes = {}, {}, {}, {}, {}, {}, {}, {}, {}
        place, sent = {}, {}

        def tile(shape, dtype, name, **kw):
            if name in place:
                return lap.tile(shape, dtype, name=name, offset=place[name], **kw)
            return sb.tile(shape, dtype, name=name, **kw)

        psum = [ps.tile([P, BANK], F32, name="bank%d" % b) for b in range(8)]

        def bank_tile(b):
            return psum[b]

        def load_list(name, src):
            lists[name] = sb.tile(list(src.shape), U16, name="list_" + name)
            nc.sync.dma_start(lists[name][:], src)

        def offsets(name, c0, c1):
            return lists[name][:, c0 // LIST_GROUP : c1 // LIST_GROUP]

        def load_half(name, src, blk, queue=nc.sync):
            dst = tile([P, PACK, P], F32, "raw_%s%d" % (name, blk))
            queue.dma_start(out=dst[:], in_=src.rearrange("(p j) n -> p j n", j=PACK)[:, :, blk * P : (blk + 1) * P])
            raw[name, blk] = dst[:]

        def load_whole(name, src, queue=nc.sync):
            dst = tile([P, PACK, N], F32, "raw_" + name)
            queue.dma_start(out=dst[:], in_=src.rearrange("(p j) n -> p j n", j=PACK))
            raw[name] = dst[:]
            for blk in range(2):
                raw[name, blk] = dst[:, :, blk * P : (blk + 1) * P]

        def gcopy(dst, src):
            nc.gpsimd.tensor_scalar(dst, src, 1.0, 0.0, MULT, ADD)

        def cast(name, blk, engine_copy):
            grouped[name, blk] = tile([P, P, PACK], BF16, "grp_%s%d" % (name, blk), align_bytes=64)
            engine_copy(
                grouped[name, blk][:].rearrange("p (c i) t -> p c t i", i=4),
                raw[name, blk].rearrange("p t (c i) -> p c t i", i=4),
            )

        def cast_on_gpsimd(name, blk):
            grouped[name, blk] = tile([P, P, PACK], BF16, "grp_%s%d" % (name, blk), align_bytes=64)
            gcopy(grouped[name, blk][:], raw[name, blk].rearrange("p t c -> p c t"))

        def quantize(name, blk):
            w_codes[name, blk] = tile([P, P], U32, "wc_%s%d" % (name, blk), align_bytes=64)[:]
            w_plane[name, blk] = tile([P, P], U8, "wp_%s%d" % (name, blk), align_bytes=64)[:]
            nc.vector.quantize_mx(
                out=w_codes[name, blk].bitcast(FP8X4),
                scales=w_plane[name, blk],
                in_=grouped[name, blk][:].rearrange("p c t -> p (c t)"),
            )

        def pick_words(c0, c1):
            half, at = divmod(c0, BANK)
            if half not in x_codes:
                x_codes[half] = tile([P, BANK], U32, "x_codes%d" % half, align_bytes=64)
            nc.vector.tensor_copy(
                x_codes[half][:, at : at + c1 - c0], word_table[:].bitcast(U32).indirect(offsets("offs", c0, c1))
            )

        def product(name, blk, c0, b, n=BANK):
            banks[name, blk, c0] = (bank_tile(b), n)
            half, at = divmod(c0, BANK)
            nc.tensor.matmul_mx(
                out=banks[name, blk, c0][0][:, 0:n],
                lhsT=w_codes[name, blk].bitcast(FP8X4),
                lhsT_scale=w_plane[name, blk],
                rhs=x_codes[half][:, at : at + n].bitcast(FP8X4),
                rhs_scale=x_plane[:, c0 : c0 + n],
                start=True,
                stop=True,
            )

        def empty(name, blk, c0, engine_copy):
            if (name, blk) not in rows:
                rows[name, blk] = tile([P, S], F32, "rows_%s%d" % (name, blk))
            bank, n = banks[name, blk, c0]
            engine_copy(rows[name, blk][:, c0 : c0 + n], bank[:, 0:n])

        def centre(name, blk, c0=0, c1=V, on_vector=False):
            if (name, blk) not in at_cen:
                at_cen[name, blk] = tile([P, V], F32, "cen_%s%d" % (name, blk))
            picked = rows[name, blk][:].indirect(offsets("cen", c0, c1))
            if on_vector:
                nc.vector.tensor_copy(at_cen[name, blk][:, c0:c1], picked)
            else:
                nc.scalar.activation(at_cen[name, blk][:, c0:c1], picked, COPY)

        def scaled(blk, d, c0=0, c1=V):
            u = tile([P, c1 - c0], F32, "u_%d%d_%d" % (blk, d, c0))[:]
            picked = rows["h", blk][:].indirect(offsets("pos%d" % (d + 1), c0, c1))
            nc.vector.tensor_tensor(u, picked, at_cen["g", blk][:, c0:c1], MULT)
            return u

        def turn(bank, src, start, stop):
            n = src.shape[1]
            for j in range(n // P):
                nc.tensor.matmul(
                    bank[:, j * P : (j + 1) * P],
                    lhsT=src[:, j * P : (j + 1) * P],
                    rhs=ident[:],
                    is_transpose=True,
                    start=start and j == 0,
                    stop=stop and j == n // P - 1,
                )

        def relu_of(z, name):
            r = tile([P, z.shape[1]], F32, name)
            nc.scalar.activation(r[:], z, RELU)
            return r

        def shifted(u, blk, c0, name, engine=nc.vector):
            n = u.shape[1]
            z = tile([P, n], F32, name)
            engine.tensor_tensor(z[:], u, at_cen["s", blk][:, c0 : c0 + n], ADD)
            return z

        def finish(z, acc, blk, c0, queue):
            n = z.shape[1]
            res = tile([P, n], F32, "res_%d_%d" % (blk, c0))
            nc.vector.scalar_tensor_tensor(res[:], z, 0.0, acc, MAX, ADD)
            queue.dma_start(out=out[blk * P : (blk + 1) * P, c0 : c0 + n], in_=res[:])

        place.update({"raw_g1": 0, "ident_raw": 1792, "raw_s0": 2048, "picked_scales": 4096, "raw_s1": 4096})
        place.update({"wc_s0": 10240, "grp_s1": 10240})
        place.update({"wp_h1": 12288, "wc_s1": 12288, "wc_h1": 14336, "u_01_0": 14336})
        place.update({"u_02_0": 14336, "u_02_256": 15360, "z12_1": 15360})
        place.update({"raw_h": 18432, "rows_g0": 18432})
        first = P - SCALE_ROWS
        scale_table = sb.tile([P, T], U8, name="scale_table")
        nc.sync.dma_start(out=scale_table[first:P, :].bitcast(I32), in_=x_scales[0].bitcast(I32))
        load_list("offs", offs)
        load_half("g", w1, 0)
        for name, src in (("cen", cen), ("pos1", pos1), ("pos2", pos2)):
            load_list(name, src)
        word_table = sb.tile([P, T], I32, name="word_table", align_bytes=64)
        nc.sync.dma_start(out=word_table[:], in_=x_words[0].rearrange("p n t -> p (n t)").bitcast(I32))
        load_whole("h", w3)

        nc.vector.memset(scale_table[0:first, :].bitcast(I32), 0)
        ident_raw = tile([P, P], F32, "ident_raw")
        make_identity(nc, ident_raw[:])
        ident = sb.tile([P, P], F32, name="ident")
        nc.scalar.activation(ident[:], ident_raw[:], RELU)
        x_plane = sb.tile([P, S], U8, name="x_plane", align_bytes=64)
        nc.vector.memset(x_plane[:].bitcast(I32), 0)

        picked_scales = tile([P, S], U8, "picked_scales", align_bytes=64)
        nc.vector.tensor_copy(picked_scales[:], scale_table[:].indirect(lists["offs"][:]))
        for q in range(4):
            nc.scalar.dma_start(
                out=x_plane[32 * q : 32 * q + 4, :].bitcast(I32),
                in_=picked_scales[first + 4 * q : first + 4 * q + 4, :].bitcast(I32),
            )
        cast("g", 0, scopy)
        quantize("g", 0)
        load_half("g", w1, 1)
        load_half("s", w2, 0)
        load_half("s", w2, 1)
        load_list("pos3", pos3)
        pick_words(0, BANK)
        pick_words(BANK, BANK + HALF)
        pick_words(BANK + HALF, S)
        cast("h", 0, scopy)
        cast_on_gpsimd("h", 1)
        product("g", 0, 0, 0)
        product("g", 0, BANK, 1, HALF)
        product("g", 0, BANK + HALF, 2, P)
        product("g", 0, S - P, 7, P)
        empty("g", 0, 0, scopy)
        empty("g", 0, BANK, scopy)
        empty("g", 0, BANK + HALF, scopy)
        empty("g", 0, S - P, scopy)
        quantize("h", 0)
        cast("g", 1, vcopy)
        quantize("h", 1)
        quantize("g", 1)
        cast("s", 0, vcopy)
        quantize("s", 0)
        for i in range(4):
            product("h", 0, i * HALF, 3 + i, HALF)
        product("g", 1, 0, 0)
        product("g", 1, BANK, 1)
        for c0 in (0, HALF):
            centre("g", 0, c0, c0 + HALF, on_vector=True)
        for i in range(4):
            empty("h", 0, i * HALF, scopy)
        product("s", 0, 0, 4)
        product("s", 0, BANK, 6)
        cast_on_gpsimd("s", 1)
        u00 = [scaled(0, 0, c0, c0 + HALF) for c0 in (0, HALF)]
        empty("g", 1, 0, scopy)
        product("h", 1, 0, 0)
        empty("g", 1, BANK, scopy)
        product("h", 1, BANK, 1)
        z0 = [bank_tile(4), bank_tile(1)]
        centre("g", 1, on_vector=True)
        quantize("s", 1)
        u01 = scaled(0, 1)
        empty("s", 0, 0, scopy)
        for i in range(2):
            turn(z0[0][:, i * HALF : (i + 1) * HALF], u00[i], i == 0, False)
        empty("s", 0, BANK, scopy)
        product("s", 1, 0, 6)
        empty("h", 1, 0, scopy)
        product("s", 1, BANK, 0)
        empty("h", 1, BANK, scopy)
        turn(z0[1], u01, True, False)
        u1 = [scaled(1, d) for d in range(3)]
        centre("s", 0)
        turn(z0[0], at_cen["s", 0][:], False, True)
        turn(z0[1], at_cen["s", 0][:], False, True)
        empty("s", 1, 0, scopy)
        empty("s", 1, BANK, scopy)
        acc0 = bank_tile(2)
        r = relu_of(z0[0][:], "r00")
        turn(acc0, r[:], True, False)
        halves = [slice(0, HALF), slice(HALF, V)]
        z1 = {(0, 0): bank_tile(6), (1, 0): bank_tile(3), (0, 1): bank_tile(0), (1, 1): bank_tile(7)}
        for d in range(2):
            for i in range(2):
                turn(z1[d, i], u1[d][:, halves[i]], True, False)
        u02 = [scaled(0, 2, i * HALF, (i + 1) * HALF) for i in range(2)]
        for i in range(2):
            centre("s", 1, i * HALF, (i + 1) * HALF)
        r = relu_of(z0[1][:], "r01")
        for d in range(2):
            turn(z1[d, 0], at_cen["s", 1][:, halves[0]], False, True)
        turn(acc0, r[:], False, True)
        for d in range(2):
            turn(z1[d, 1], at_cen["s", 1][:, halves[1]], False, True)
        acc1 = [bank_tile(4), bank_tile(1)]
        for i in range(2):
            for d in range(2):
                r = relu_of(z1[d, i][:, 0:HALF], "r1%d_%d" % (d, i))
                turn(acc1[i], r[:], d == 0, d == 1)
        z12_lo = shifted(u1[2][:, halves[0]], 1, 0, "z12_0")
        z02 = [shifted(u02[i], 0, i * HALF, "z02_%d" % i) for i in range(2)]
        for i in range(2):
            finish(z02[i][:], acc0[:, halves[i]], 0, i * HALF, nc.sync)
        z12_hi = shifted(u1[2][:, halves[1]], 1, HALF, "z12_1", nc.gpsimd)
        finish(z12_lo[:], acc1[0][:, 0:HALF], 1, 0, nc.sync)
        finish(z12_hi[:], acc1[1][:, 0:HALF], 1, HALF, nc.sync)
